import numpy as np
import ml_dtypes


def mxq(x, axis, fmt="e4m3"):
    dtype, down = {"e4m3": (ml_dtypes.float8_e4m3fn, 7), "e5m2": (ml_dtypes.float8_e5m2, 14)}[fmt]
    v = np.moveaxis(np.asarray(x, np.float32).astype(ml_dtypes.bfloat16).astype(np.float64), axis, -1)
    blocks = v.reshape(v.shape[:-1] + (-1, 32))
    amax = np.abs(blocks).max(-1, keepdims=True)
    byte = np.maximum(np.where(amax > 0, np.frexp(amax)[1] - 1 + 127, 0) - down, 1)
    scale = np.exp2(byte - 127.0)
    codes = (blocks / scale).astype(np.float32).astype(dtype).astype(np.float64)
    return np.moveaxis((codes * scale).reshape(v.shape), -1, axis)


WIDE = False


def mx_kscale(k):
    if not WIDE:
        return np.ones(k)
    levels = np.array([24, -24, 12, -12, 0])
    if k % 512:
        return np.exp2(np.random.permutation(np.resize(levels, k // 32))).repeat(32)
    a = np.empty((k // 512, 16))
    for p in range(k // 512):
        a[p, :8] = np.random.permutation(np.resize(levels, 8))
        for g in range(8):
            far = levels[np.abs(levels - a[p, g]) >= 10]
            a[p, g + 8] = far[np.random.randint(len(far))]
    return np.exp2(a.ravel()).repeat(32)


def f64(x):
    return np.asarray(x).astype(np.float64)


def striped8(idx):
    return np.concatenate([v.reshape(-1, 16).T for v in idx]).astype(np.uint16)


def unstriped8(offs):
    return np.stack([offs[16 * g:16 * g + 16].T.reshape(-1) for g in range(8)]).astype(np.int64)


E2M1 = np.array([0.0, 0.5, 1.0, 1.5, 2.0, 3.0, 4.0, 6.0, -0.0, -0.5, -1.0, -1.5, -2.0, -3.0, -4.0, -6.0])


def pack_weight(w, fmt):
    k, n = w.shape
    w = f64(np.asarray(w, np.float32).astype(ml_dtypes.bfloat16)).reshape(k // 32, 32, n)
    amax = np.abs(w).max(1)
    if fmt == "e4m3":
        byte = np.frexp(amax)[1] - 1 + 127 - 7
    else:
        mant, ex = np.frexp(amax / 6.0)
        byte = np.where(mant > 0.5, ex, ex - 1) + 127
    byte = np.clip(np.where(amax > 0, byte, 1), 1, 254)
    scaled = (w * np.exp2(127.0 - byte)[:, None, :]).reshape(k, n).astype(np.float32)
    by_word = np.ascontiguousarray(scaled.reshape(k // 512, 128, 4, n).transpose(0, 1, 3, 2))
    if fmt == "e4m3":
        words = by_word.astype(ml_dtypes.float8_e4m3fn).view(np.uint8)
    else:
        c = by_word.astype(ml_dtypes.float4_e2m1fn).view(np.uint8) & 0xF
        words = (c[..., 0::2] | (c[..., 1::2] << 4)).reshape(k // 512, 128, 2 * n)
    return np.ascontiguousarray(words), np.ascontiguousarray(byte.astype(np.uint8).reshape(k // 512, 16, n))


def unpack_weight(words, scales, fmt):
    g, _, n = scales.shape
    words = np.ascontiguousarray(words).reshape(g, 128, n, -1)
    if fmt == "e4m3":
        vals = words.view(ml_dtypes.float8_e4m3fn).astype(np.float64)
    else:
        nib = np.empty((g, 128, n, 4), np.uint8)
        nib[..., 0::2] = words & 0xF
        nib[..., 1::2] = words >> 4
        vals = E2M1[nib]
    vals = vals * np.repeat(np.exp2(scales.astype(np.float64) - 127.0), 8, axis=1)[..., None]
    return vals.transpose(0, 1, 3, 2).reshape(g * 512, n)


def gelu(f):
    return 0.5 * f * (1.0 + np.tanh(np.sqrt(2.0 / np.pi) * (f + 0.044715 * f**3)))


K, N, T, J = 512, 512, 2048, 512


def setup_inputs():
    n = np.random.standard_normal
    s = mx_kscale(K)[:, None]
    p_w4 = pack_weight(n((K, N)) / np.sqrt(K) / s, "e2m1")
    return {
        "xT": (n((K, T)) * s).astype(np.float32),
        "wgt": np.repeat(np.random.uniform(0.5, 2.0, (8, 2 * J)), 16, axis=0).astype(np.float32),
        "w4_words": p_w4[0],
        "w4_scales": p_w4[1],
        "wd": (0.4 * (n((K, N)) / np.sqrt(K) / s)).astype(np.float32),
        "b": (0.3 * n(N)).astype(np.float32),
        "offs": striped8(np.stack([np.concatenate([np.random.permutation(T)[:J] for _ in range(2)]) for _ in range(8)])),
    }


def reference(xT, wgt, w4_words, w4_scales, wd, b, offs):
    idx = unstriped8(offs)
    rows = np.arange(K)
    xg = f64(wgt)[rows // 4 % 128] * f64(xT)[rows[:, None], idx[rows % 512 // 64]]
    xT_ = mxq(xg, 0, "e4m3").reshape(K, 2, J)
    w4_ = unpack_weight(w4_words, w4_scales, "e2m1")
    wd_ = mxq(f64(wd), 0, "e4m3")
    a0 = w4_.T @ xT_[:, 0] + wd_.T @ xT_[:, 0]
    a1 = w4_.T @ xT_[:, 1] + wd_.T @ xT_[:, 1]
    return gelu(a0 * a1 + f64(b)[:, None])

@@ -1,0 +1,160 @@
+from contextlib import ExitStack
+
+import concourse.mybir as mybir
+
+K, N, T, J = 512, 512, 2048, 512
+FLOPS = 2 * 2 * 2 * K * N * J
+
+F32 = mybir.dt.float32
+BF16 = mybir.dt.bfloat16
+I32 = mybir.dt.int32
+U32 = mybir.dt.uint32
+U16 = mybir.dt.uint16
+U8 = mybir.dt.uint8
+FP8X4 = mybir.dt.float8_e4m3fn_x4
+FP4X4 = mybir.dt.float4_e2m1fn_x4
+MULT = mybir.AluOpType.mult
+GELU = mybir.ActivationFunctionType.Gelu_apprx_tanh
+
+P = 128
+PACK = 4
+PICKS = 2
+HALF = 256
+RUN = 4
+
+
+def tile_list_dl_prod_gelu_kernel(tc, xT, wgt, w4_words, w4_scales, wd, b, offs, out):
+    nc = tc.nc
+    with ExitStack() as ctx:
+        pool = ctx.enter_context(tc.tile_pool(name="sbuf", bufs=1))
+        psum = ctx.enter_context(tc.psum_pool(name="psum", bufs=1))
+
+        offsets = pool.tile([P, PICKS * J // 16], U16, name="offsets")
+        weight = [pool.tile([P, J], F32, name="weight%d" % c) for c in range(PICKS)]
+        plane = [pool.tile([P, T], F32, name="plane%d" % t) for t in range(PACK)]
+        w4_codes = pool.tile([P, 2 * N], U8, name="w4_codes", align_bytes=64)
+        w4_scale = pool.tile([P, N], U8, name="w4_scale", align_bytes=64)
+        bias = pool.tile([P, N // P], F32, name="bias")
+        wd_raw = [pool.tile([P, PACK, HALF], F32, name="wd_raw%d" % u) for u in range(2)]
+        wd_bf = [pool.tile([P, HALF, PACK], BF16, name="wd_bf%d" % u, align_bytes=64) for u in range(2)]
+        wd_codes = [pool.tile([P, HALF], U32, name="wd_codes%d" % u, align_bytes=64) for u in range(2)]
+        wd_scale = [pool.tile([P, HALF], U8, name="wd_scale%d" % u, align_bytes=64) for u in range(2)]
+        picked = [pool.tile([P, PACK, J], F32, name="picked%d" % c) for c in range(PICKS)]
+        x_bf = [pool.tile([P, PICKS * HALF, PACK], BF16, name="x_bf%d" % h, align_bytes=64) for h in range(2)]
+        x_codes = [pool.tile([P, PICKS * HALF], U32, name="x_codes%d" % h, align_bytes=64) for h in range(2)]
+        x_scale = [pool.tile([P, PICKS * HALF], U8, name="x_scale%d" % h, align_bytes=64) for h in range(2)]
+        acc = {(h, m): psum.tile([P, PICKS * HALF], F32, name="acc%d_%d" % (h, m)) for h in range(2) for m in range(4)}
+
+        x_rows = xT.rearrange("(p t) c -> p t c", t=PACK)
+        wd_rows = wd.rearrange("(p t) n -> p t n", t=PACK)
+
+        nc.vector.memset(w4_scale[:].bitcast(I32), 0)
+        nc.sync.dma_start(offsets[:], offs)
+        nc.sync.dma_start(weight[0][:], wgt[:, 0:J])
+        nc.sync.dma_start(plane[0][:], x_rows[:, 0, :])
+        for q in range(4):
+            nc.sync.dma_start(
+                w4_scale[:].bitcast(I32)[32 * q : 32 * q + 4, :],
+                w4_scales[0].bitcast(I32)[4 * q : 4 * q + 4, :],
+            )
+        with nc.allow_non_contiguous_dma(reason="one bias value to a partition"):
+            nc.sync.dma_start(bias[:], b.rearrange("(m p) -> p m", p=P))
+        nc.sync.dma_start(weight[1][:], wgt[:, J : 2 * J])
+        for t in range(1, PACK):
+            nc.sync.dma_start(plane[t][:], x_rows[:, t, :])
+        nc.sync.dma_start(wd_raw[0][:], wd_rows[:, :, 0:HALF])
+        nc.sync.dma_start(w4_codes[:].bitcast(I32), w4_words[0].bitcast(I32))
+        nc.sync.dma_start(wd_raw[1][:], wd_rows[:, :, HALF:N])
+
+        warm = pool.tile([P, 1], F32, name="warm")
+        nc.scalar.activation(warm[:], bias[:, 0:1], GELU)
+
+        def gather(t, c, j0, j1):
+            cols = offsets[:, (c * J + j0) // 16 : (c * J + j1) // 16]
+            nc.vector.tensor_tensor(picked[c][:, t, j0:j1], plane[t][:].indirect(cols), weight[c][:, j0:j1], MULT)
+
+        def interleave(on_scalar, dst, src):
+            dst = dst.rearrange("p (g i) t -> p g t i", i=RUN)
+            src = src.rearrange("p t (g i) -> p g t i", i=RUN)
+            if on_scalar:
+                nc.scalar.copy(dst, src)
+            else:
+                nc.vector.tensor_copy(dst, src)
+
+        def interleave_x(on_scalar, h, c, j0, j1):
+            interleave(on_scalar, x_bf[h][:, c * HALF + j0 : c * HALF + j1, :], picked[c][:, :, h * HALF + j0 : h * HALF + j1])
+
+        def quantize(codes, scale, src, w0, w1):
+            nc.vector.quantize_mx(codes[:, w0:w1].bitcast(FP8X4), scale[:, w0:w1], src[:, w0:w1, :].rearrange("p w t -> p (w t)"))
+
+        def pass_w4(h, m):
+            nc.tensor.matmul_mx(
+                acc[h, m][:],
+                lhsT=w4_codes[:, 2 * P * m : 2 * P * (m + 1)].bitcast(FP4X4),
+                lhsT_scale=w4_scale[:, P * m : P * (m + 1)],
+                rhs=x_codes[h][:].bitcast(FP8X4),
+                rhs_scale=x_scale[h][:],
+                start=True,
+                stop=False,
+            )
+
+        def pass_wd(h, m):
+            u, cols = m // 2, slice(P * (m % 2), P * (m % 2 + 1))
+            nc.tensor.matmul_mx(
+                acc[h, m][:],
+                lhsT=wd_codes[u][:, cols].bitcast(FP8X4),
+                lhsT_scale=wd_scale[u][:, cols],
+                rhs=x_codes[h][:].bitcast(FP8X4),
+                rhs_scale=x_scale[h][:],
+                start=False,
+                stop=True,
+            )
+
+        def finish(h, m, on_scalar):
+            first = pool.tile([P, HALF], F32, name="first%d_%d" % (h, m))
+            prod = pool.tile([P, HALF], F32, name="prod%d_%d" % (h, m))
+            res = pool.tile([P, HALF], F32, name="res%d_%d" % (h, m))
+            if on_scalar:
+                nc.scalar.copy(first[:], acc[h, m][:, 0:HALF])
+            else:
+                nc.vector.tensor_copy(first[:], acc[h, m][:, 0:HALF])
+            nc.vector.tensor_tensor(prod[:], acc[h, m][:, HALF : 2 * HALF], first[:], MULT)
+            nc.scalar.activation(res[:], prod[:], GELU, bias=bias[:, m : m + 1])
+            nc.sync.dma_start(out[P * m : P * (m + 1), h * HALF : (h + 1) * HALF], res[:])
+
+        for t in range(PACK - 1):
+            for c in range(PICKS):
+                gather(t, c, 0, J)
+        last = PACK - 1
+        Q = HALF // 2
+
+        def quantize_x(h):
+            quantize(x_codes[h], x_scale[h], x_bf[h], HALF, HALF + Q)
+            quantize(x_codes[h], x_scale[h], x_bf[h], 0, HALF)
+            quantize(x_codes[h], x_scale[h], x_bf[h], HALF + Q, 2 * HALF)
+
+        gather(last, 0, 0, HALF)
+        interleave_x(True, 0, 0, 0, HALF)
+        gather(last, 1, 0, Q)
+        gather(last, 1, Q, HALF)
+        interleave_x(False, 0, 1, 0, Q)
+        interleave_x(False, 0, 1, Q, HALF)
+        quantize_x(0)
+        interleave(True, wd_bf[0][:], wd_raw[0][:])
+        gather(last, 0, HALF, J)
+        quantize(wd_codes[0], wd_scale[0], wd_bf[0], 0, HALF)
+        interleave(True, wd_bf[1][:], wd_raw[1][:])
+        interleave_x(True, 1, 0, 0, HALF)
+        gather(last, 1, HALF, HALF + Q)
+        gather(last, 1, HALF + Q, J)
+        quantize(wd_codes[1], wd_scale[1], wd_bf[1], 0, HALF)
+        interleave_x(False, 1, 1, 0, Q)
+        interleave_x(False, 1, 1, Q, HALF)
+        quantize_x(1)
+        for h in range(2):
+            for m in range(4):
+                pass_w4(h, m)
+                pass_wd(h, m)
+        for h in range(2):
+            for m in range(4):
+                finish(h, m, h == 0 or m % 2 == 1)

@@ -1,6 +1,7 @@
 from contextlib import ExitStack
 
 import concourse.mybir as mybir
+from concourse.masks import make_identity
 
 K, N, T, J = 512, 512, 2048, 512
 FLOPS = 2 * 2 * 2 * K * N * J
@@ -30,7 +31,7 @@ def tile_list_dl_prod_gelu_kernel(tc, xT, wgt, w4_words, w4_scales, wd, b, offs,
         psum = ctx.enter_context(tc.psum_pool(name="psum", bufs=1))
 
         offsets = pool.tile([P, PICKS * J // 16], U16, name="offsets")
-        weight = [pool.tile([P, J], F32, name="weight%d" % c) for c in range(PICKS)]
+        weight = [pool.tile([P, J], F32, name="weight%d" % c, align_bytes=64) for c in range(PICKS)]
         plane = [pool.tile([P, T], F32, name="plane%d" % t) for t in range(PACK)]
         w4_codes = pool.tile([P, 2 * N], U8, name="w4_codes", align_bytes=64)
         w4_scale = pool.tile([P, N], U8, name="w4_scale", align_bytes=64)
@@ -49,25 +50,37 @@ def tile_list_dl_prod_gelu_kernel(tc, xT, wgt, w4_words, w4_scales, wd, b, offs,
         wd_rows = wd.rearrange("(p t) n -> p t n", t=PACK)
 
         nc.vector.memset(w4_scale[:].bitcast(I32), 0)
-        nc.sync.dma_start(offsets[:], offs)
         nc.sync.dma_start(weight[0][:], wgt[:, 0:J])
+        rows = pool.tile([P, 2, 32], F32, name="rows", align_bytes=64)
+        cols = pool.tile([P, 2, 32], F32, name="cols", align_bytes=64)
+        spread = pool.tile([P, 16, 2, 16], F32, name="spread", align_bytes=64)
+        for q in range(4):
+            nc.sync.dma_start(rows[32 * q : 32 * q + 32, :, :], wgt[32 * q : 32 * q + 32 : 16, :].rearrange("g (r c) -> r g c", c=32))
+        for g in range(2):
+            nc.vector.transpose(cols[:, g, :], rows[:, g, :])
+        nc.vector.tensor_copy(spread[:], cols[:, :, 16:32].rearrange("p g r -> p r g").unsqueeze(3).to_broadcast([P, 16, 2, 16]))
+        nc.vector.transpose(weight[1][:], spread[:].rearrange("p r g a -> p (r g a)"))
         nc.sync.dma_start(plane[0][:], x_rows[:, 0, :])
+        nc.sync.dma_start(offsets[:], offs)
+        for t in range(1, PACK):
+            nc.sync.dma_start(plane[t][:], x_rows[:, t, :])
+        nc.sync.dma_start(w4_codes[:].bitcast(I32), w4_words[0].bitcast(I32))
+        nc.sync.dma_start(wd_raw[0][:], wd_rows[:, :, 0:HALF])
         for q in range(4):
             nc.sync.dma_start(
                 w4_scale[:].bitcast(I32)[32 * q : 32 * q + 4, :],
                 w4_scales[0].bitcast(I32)[4 * q : 4 * q + 4, :],
             )
+        nc.sync.dma_start(wd_raw[1][:], wd_rows[:, :, HALF:N])
         with nc.allow_non_contiguous_dma(reason="one bias value to a partition"):
             nc.sync.dma_start(bias[:], b.rearrange("(m p) -> p m", p=P))
-        nc.sync.dma_start(weight[1][:], wgt[:, J : 2 * J])
-        for t in range(1, PACK):
-            nc.sync.dma_start(plane[t][:], x_rows[:, t, :])
-        nc.sync.dma_start(wd_raw[0][:], wd_rows[:, :, 0:HALF])
-        nc.sync.dma_start(w4_codes[:].bitcast(I32), w4_words[0].bitcast(I32))
-        nc.sync.dma_start(wd_raw[1][:], wd_rows[:, :, HALF:N])
 
+        zero = pool.tile([P, 1], F32, name="zero")
         warm = pool.tile([P, 1], F32, name="warm")
-        nc.scalar.activation(warm[:], bias[:, 0:1], GELU)
+        nc.vector.memset(zero[:], 0.0)
+        nc.scalar.activation(warm[:], zero[:], GELU)
+        ident = pool.tile([P, P], BF16, name="ident")
+        make_identity(nc, ident[:])
 
         def gather(t, c, j0, j1):
             cols = offsets[:, (c * J + j0) // 16 : (c * J + j1) // 16]
@@ -81,8 +94,14 @@ def tile_list_dl_prod_gelu_kernel(tc, xT, wgt, w4_words, w4_scales, wd, b, offs,
             else:
                 nc.vector.tensor_copy(dst, src)
 
-        def interleave_x(on_scalar, h, c, j0, j1):
-            interleave(on_scalar, x_bf[h][:, c * HALF + j0 : c * HALF + j1, :], picked[c][:, :, h * HALF + j0 : h * HALF + j1])
+        def interleave_x(on_scalar, pair, h, c, j0, j1):
+            planes = slice(2 * pair, 2 * pair + 2)
+            dst = x_bf[h][:, c * HALF + j0 : c * HALF + j1, planes]
+            src = picked[c][:, planes, h * HALF + j0 : h * HALF + j1].rearrange("p t w -> p w t")
+            if on_scalar:
+                nc.scalar.copy(dst, src)
+            else:
+                nc.vector.tensor_copy(dst, src)
 
         def quantize(codes, scale, src, w0, w1):
             nc.vector.quantize_mx(codes[:, w0:w1].bitcast(FP8X4), scale[:, w0:w1], src[:, w0:w1, :].rearrange("p w t -> p (w t)"))
@@ -110,51 +129,62 @@ def tile_list_dl_prod_gelu_kernel(tc, xT, wgt, w4_words, w4_scales, wd, b, offs,
                 stop=True,
             )
 
-        def finish(h, m, on_scalar):
-            first = pool.tile([P, HALF], F32, name="first%d_%d" % (h, m))
-            prod = pool.tile([P, HALF], F32, name="prod%d_%d" % (h, m))
-            res = pool.tile([P, HALF], F32, name="res%d_%d" % (h, m))
+        def finish(h, m, on_scalar, j0, j1):
+            w = j1 - j0
+            first = pool.tile([P, w], F32, name="first%d_%d_%d" % (h, m, j0))
+            prod = pool.tile([P, w], F32, name="prod%d_%d_%d" % (h, m, j0))
+            res = pool.tile([P, w], F32, name="res%d_%d_%d" % (h, m, j0))
             if on_scalar:
-                nc.scalar.copy(first[:], acc[h, m][:, 0:HALF])
+                nc.scalar.copy(first[:], acc[h, m][:, j0:j1])
             else:
-                nc.vector.tensor_copy(first[:], acc[h, m][:, 0:HALF])
-            nc.vector.tensor_tensor(prod[:], acc[h, m][:, HALF : 2 * HALF], first[:], MULT)
+                nc.vector.tensor_copy(first[:], acc[h, m][:, j0:j1])
+            nc.vector.tensor_tensor(prod[:], acc[h, m][:, HALF + j0 : HALF + j1], first[:], MULT)
             nc.scalar.activation(res[:], prod[:], GELU, bias=bias[:, m : m + 1])
-            nc.sync.dma_start(out[P * m : P * (m + 1), h * HALF : (h + 1) * HALF], res[:])
+            nc.sync.dma_start(out[P * m : P * (m + 1), h * HALF + j0 : h * HALF + j1], res[:])
 
         for t in range(PACK - 1):
             for c in range(PICKS):
                 gather(t, c, 0, J)
+                if t == 1:
+                    for h in range(2):
+                        interleave_x(True, 0, h, c, 0, HALF)
+        warm_src = pool.tile([P, P], BF16, name="warm_src")
+        nc.scalar.copy(warm_src[:], picked[0][:, PACK - 2, 0:P])
+        warm_dst = acc[1, 3][:].bitcast(BF16)
+        for i in range(24):
+            nc.tensor.transpose(warm_dst[:, P * (i % 8) : P * (i % 8 + 1)], warm_src[:], ident[:])
         last = PACK - 1
         Q = HALF // 2
-
-        def quantize_x(h):
-            quantize(x_codes[h], x_scale[h], x_bf[h], HALF, HALF + Q)
-            quantize(x_codes[h], x_scale[h], x_bf[h], 0, HALF)
-            quantize(x_codes[h], x_scale[h], x_bf[h], HALF + Q, 2 * HALF)
-
-        gather(last, 0, 0, HALF)
-        interleave_x(True, 0, 0, 0, HALF)
-        gather(last, 1, 0, Q)
-        gather(last, 1, Q, HALF)
-        interleave_x(False, 0, 1, 0, Q)
-        interleave_x(False, 0, 1, Q, HALF)
-        quantize_x(0)
+        for j0 in (0, Q):
+            gather(last, 0, j0, j0 + Q)
+            interleave_x(True, 1, 0, 0, j0, j0 + Q)
+        for j0 in (0, Q):
+            gather(last, 1, j0, j0 + Q)
+        for j0 in (0, Q):
+            interleave_x(False, 1, 0, 1, j0, j0 + Q)
+        for w0 in (0, HALF, Q, HALF + Q):
+            quantize(x_codes[0], x_scale[0], x_bf[0], w0, w0 + Q)
         interleave(True, wd_bf[0][:], wd_raw[0][:])
         gather(last, 0, HALF, J)
         quantize(wd_codes[0], wd_scale[0], wd_bf[0], 0, HALF)
         interleave(True, wd_bf[1][:], wd_raw[1][:])
-        interleave_x(True, 1, 0, 0, HALF)
+        interleave_x(True, 1, 1, 0, 0, HALF)
         gather(last, 1, HALF, HALF + Q)
+        interleave_x(True, 1, 1, 1, 0, Q)
         gather(last, 1, HALF + Q, J)
         quantize(wd_codes[1], wd_scale[1], wd_bf[1], 0, HALF)
-        interleave_x(False, 1, 1, 0, Q)
-        interleave_x(False, 1, 1, Q, HALF)
-        quantize_x(1)
+        interleave_x(False, 1, 1, 1, Q, HALF)
+        for w0, w1 in ((0, HALF), (HALF, HALF + Q), (HALF + Q, 2 * HALF)):
+            quantize(x_codes[1], x_scale[1], x_bf[1], w0, w1)
         for h in range(2):
             for m in range(4):
                 pass_w4(h, m)
                 pass_wd(h, m)
         for h in range(2):
             for m in range(4):
-                finish(h, m, h == 0 or m % 2 == 1)
+                on_scalar = h == 0 or m == 2
+                if (h, m) == (1, 3):
+                    for j0 in (0, Q):
+                        finish(h, m, on_scalar, j0, j0 + Q)
+                else:
+                    finish(h, m, on_scalar, 0, HALF)

@@ -1,7 +1,6 @@
 from contextlib import ExitStack
 
 import concourse.mybir as mybir
-from concourse.masks import make_identity
 
 K, N, T, J = 512, 512, 2048, 512
 FLOPS = 2 * 2 * 2 * K * N * J
@@ -62,15 +61,16 @@ def tile_list_dl_prod_gelu_kernel(tc, xT, wgt, w4_words, w4_scales, wd, b, offs,
         nc.vector.transpose(weight[1][:], spread[:].rearrange("p r g a -> p (r g a)"))
         nc.sync.dma_start(plane[0][:], x_rows[:, 0, :])
         nc.sync.dma_start(offsets[:], offs)
-        for t in range(1, PACK):
+        for t in range(1, PACK - 1):
             nc.sync.dma_start(plane[t][:], x_rows[:, t, :])
-        nc.sync.dma_start(w4_codes[:].bitcast(I32), w4_words[0].bitcast(I32))
-        nc.sync.dma_start(wd_raw[0][:], wd_rows[:, :, 0:HALF])
         for q in range(4):
             nc.sync.dma_start(
                 w4_scale[:].bitcast(I32)[32 * q : 32 * q + 4, :],
                 w4_scales[0].bitcast(I32)[4 * q : 4 * q + 4, :],
             )
+        nc.sync.dma_start(plane[PACK - 1][:], x_rows[:, PACK - 1, :])
+        nc.sync.dma_start(w4_codes[:].bitcast(I32), w4_words[0].bitcast(I32))
+        nc.sync.dma_start(wd_raw[0][:], wd_rows[:, :, 0:HALF])
         nc.sync.dma_start(wd_raw[1][:], wd_rows[:, :, HALF:N])
         with nc.allow_non_contiguous_dma(reason="one bias value to a partition"):
             nc.sync.dma_start(bias[:], b.rearrange("(m p) -> p m", p=P))
@@ -79,8 +79,6 @@ def tile_list_dl_prod_gelu_kernel(tc, xT, wgt, w4_words, w4_scales, wd, b, offs,
         warm = pool.tile([P, 1], F32, name="warm")
         nc.vector.memset(zero[:], 0.0)
         nc.scalar.activation(warm[:], zero[:], GELU)
-        ident = pool.tile([P, P], BF16, name="ident")
-        make_identity(nc, ident[:])
 
         def gather(t, c, j0, j1):
             cols = offsets[:, (c * J + j0) // 16 : (c * J + j1) // 16]
@@ -148,11 +146,6 @@ def tile_list_dl_prod_gelu_kernel(tc, xT, wgt, w4_words, w4_scales, wd, b, offs,
                 if t == 1:
                     for h in range(2):
                         interleave_x(True, 0, h, c, 0, HALF)
-        warm_src = pool.tile([P, P], BF16, name="warm_src")
-        nc.scalar.copy(warm_src[:], picked[0][:, PACK - 2, 0:P])
-        warm_dst = acc[1, 3][:].bitcast(BF16)
-        for i in range(24):
-            nc.tensor.transpose(warm_dst[:, P * (i % 8) : P * (i % 8 + 1)], warm_src[:], ident[:])
         last = PACK - 1
         Q = HALF // 2
         for j0 in (0, Q):

@@ -153,9 +153,20 @@ def tile_list_dl_prod_gelu_kernel(tc, xT, wgt, w4_words, w4_scales, wd, b, offs,
             interleave_x(True, 1, 0, 0, j0, j0 + Q)
         for j0 in (0, Q):
             gather(last, 1, j0, j0 + Q)
+        quantize(x_codes[0], x_scale[0], x_bf[0], 0, Q)
+        for i in range(4):
+            nc.tensor.matmul_mx(
+                acc[1, 3][:, P * (i % 4) : P * (i % 4 + 1)],
+                lhsT=w4_codes[:, 0 : 2 * P].bitcast(FP4X4),
+                lhsT_scale=w4_scale[:, 0:P],
+                rhs=x_codes[0][:, 0:Q].bitcast(FP8X4),
+                rhs_scale=x_scale[0][:, 0:Q],
+                start=True,
+                stop=True,
+            )
         for j0 in (0, Q):
             interleave_x(False, 1, 0, 1, j0, j0 + Q)
-        for w0 in (0, HALF, Q, HALF + Q):
+        for w0 in (HALF, Q, HALF + Q):
             quantize(x_codes[0], x_scale[0], x_bf[0], w0, w0 + Q)
         interleave(True, wd_bf[0][:], wd_raw[0][:])
         gather(last, 0, HALF, J)

@@ -14,6 +14,7 @@ U8 = mybir.dt.uint8
 FP8X4 = mybir.dt.float8_e4m3fn_x4
 FP4X4 = mybir.dt.float4_e2m1fn_x4
 MULT = mybir.AluOpType.mult
+AX = mybir.AxisListType.X
 GELU = mybir.ActivationFunctionType.Gelu_apprx_tanh
 
 P = 128
@@ -21,6 +22,12 @@ PACK = 4
 PICKS = 2
 HALF = 256
 RUN = 4
+W = 128
+WIDTH = [128] * 4
+START = [sum(WIDTH[:c]) for c in range(len(WIDTH))]
+CHUNKS = len(WIDTH)
+PARTS = [2, 2]
+PSTART = [sum(PARTS[:u]) for u in range(len(PARTS))]
 
 
 def tile_list_dl_prod_gelu_kernel(tc, xT, wgt, w4_words, w4_scales, wd, b, offs, out):
@@ -30,165 +37,308 @@ def tile_list_dl_prod_gelu_kernel(tc, xT, wgt, w4_words, w4_scales, wd, b, offs,
         psum = ctx.enter_context(tc.psum_pool(name="psum", bufs=1))
 
         offsets = pool.tile([P, PICKS * J // 16], U16, name="offsets")
-        weight = [pool.tile([P, J], F32, name="weight%d" % c, align_bytes=64) for c in range(PICKS)]
+        weight = [pool.tile([P, J], F32, name="weight%d" % k, align_bytes=64) for k in range(PICKS)]
         plane = [pool.tile([P, T], F32, name="plane%d" % t) for t in range(PACK)]
         w4_codes = pool.tile([P, 2 * N], U8, name="w4_codes", align_bytes=64)
         w4_scale = pool.tile([P, N], U8, name="w4_scale", align_bytes=64)
         bias = pool.tile([P, N // P], F32, name="bias")
-        wd_raw = [pool.tile([P, PACK, HALF], F32, name="wd_raw%d" % u) for u in range(2)]
-        wd_bf = [pool.tile([P, HALF, PACK], BF16, name="wd_bf%d" % u, align_bytes=64) for u in range(2)]
-        wd_codes = [pool.tile([P, HALF], U32, name="wd_codes%d" % u, align_bytes=64) for u in range(2)]
-        wd_scale = [pool.tile([P, HALF], U8, name="wd_scale%d" % u, align_bytes=64) for u in range(2)]
-        picked = [pool.tile([P, PACK, J], F32, name="picked%d" % c) for c in range(PICKS)]
-        x_bf = [pool.tile([P, PICKS * HALF, PACK], BF16, name="x_bf%d" % h, align_bytes=64) for h in range(2)]
-        x_codes = [pool.tile([P, PICKS * HALF], U32, name="x_codes%d" % h, align_bytes=64) for h in range(2)]
-        x_scale = [pool.tile([P, PICKS * HALF], U8, name="x_scale%d" % h, align_bytes=64) for h in range(2)]
-        acc = {(h, m): psum.tile([P, PICKS * HALF], F32, name="acc%d_%d" % (h, m)) for h in range(2) for m in range(4)}
+        OWN = 3 * 8
+        RAW = OWN + 8
+        stage = pool.tile([P, (RAW + 16) * W], F32, name="stage")
+        blocks = stage[:].rearrange("p (x w) -> p x w", w=W)
+        wd_raw = [stage[:, (RAW + 4 * PSTART[u]) * W : (RAW + 4 * (PSTART[u] + n)) * W].rearrange("p (t n) -> p t n", t=PACK) for u, n in enumerate(PARTS)]
+        wd_bf = [pool.tile([P, n * P, PACK], BF16, name="wd_bf%d" % u, align_bytes=64) for u, n in enumerate(PARTS)]
+        wd_codes = [pool.tile([P, n * P], U32, name="wd_codes%d" % u, align_bytes=64) for u, n in enumerate(PARTS)]
+        wd_scale = [pool.tile([P, n * P], U8, name="wd_scale%d" % u, align_bytes=64) for u, n in enumerate(PARTS)]
+        x_bf = [pool.tile([P, PICKS * WIDTH[c], PACK], BF16, name="x_bf%d" % c, align_bytes=64) for c in range(CHUNKS)]
+        x_codes = [pool.tile([P, PICKS * WIDTH[c]], U32, name="x_codes%d" % c, align_bytes=64) for c in range(CHUNKS)]
+        x_scale = [pool.tile([P, PICKS * WIDTH[c]], U8, name="x_scale%d" % c, align_bytes=64) for c in range(CHUNKS)]
+        bank = {}
+        for c in range(CHUNKS):
+            for h in range(2 * WIDTH[c] // W):
+                bank[c, h] = psum.tile([P, 4 * W], F32, name="bank%d_%d" % (c, h))
 
         x_rows = xT.rearrange("(p t) c -> p t c", t=PACK)
         wd_rows = wd.rearrange("(p t) n -> p t n", t=PACK)
+        out_rows = out.rearrange("(m p) j -> p m j", p=P)
 
         nc.vector.memset(w4_scale[:].bitcast(I32), 0)
-        nc.sync.dma_start(weight[0][:], wgt[:, 0:J])
-        rows = pool.tile([P, 2, 32], F32, name="rows", align_bytes=64)
-        cols = pool.tile([P, 2, 32], F32, name="cols", align_bytes=64)
-        spread = pool.tile([P, 16, 2, 16], F32, name="spread", align_bytes=64)
-        for q in range(4):
-            nc.sync.dma_start(rows[32 * q : 32 * q + 32, :, :], wgt[32 * q : 32 * q + 32 : 16, :].rearrange("g (r c) -> r g c", c=32))
-        for g in range(2):
-            nc.vector.transpose(cols[:, g, :], rows[:, g, :])
-        nc.vector.tensor_copy(spread[:], cols[:, :, 16:32].rearrange("p g r -> p r g").unsqueeze(3).to_broadcast([P, 16, 2, 16]))
-        nc.vector.transpose(weight[1][:], spread[:].rearrange("p r g a -> p (r g a)"))
-        nc.sync.dma_start(plane[0][:], x_rows[:, 0, :])
-        nc.sync.dma_start(offsets[:], offs)
-        for t in range(1, PACK - 1):
-            nc.sync.dma_start(plane[t][:], x_rows[:, t, :])
-        for q in range(4):
-            nc.sync.dma_start(
-                w4_scale[:].bitcast(I32)[32 * q : 32 * q + 4, :],
-                w4_scales[0].bitcast(I32)[4 * q : 4 * q + 4, :],
-            )
-        nc.sync.dma_start(plane[PACK - 1][:], x_rows[:, PACK - 1, :])
-        nc.sync.dma_start(w4_codes[:].bitcast(I32), w4_words[0].bitcast(I32))
-        nc.sync.dma_start(wd_raw[0][:], wd_rows[:, :, 0:HALF])
-        nc.sync.dma_start(wd_raw[1][:], wd_rows[:, :, HALF:N])
-        with nc.allow_non_contiguous_dma(reason="one bias value to a partition"):
-            nc.sync.dma_start(bias[:], b.rearrange("(m p) -> p m", p=P))
-
         zero = pool.tile([P, 1], F32, name="zero")
         warm = pool.tile([P, 1], F32, name="warm")
         nc.vector.memset(zero[:], 0.0)
         nc.scalar.activation(warm[:], zero[:], GELU)
 
-        def gather(t, c, j0, j1):
-            cols = offsets[:, (c * J + j0) // 16 : (c * J + j1) // 16]
-            nc.vector.tensor_tensor(picked[c][:, t, j0:j1], plane[t][:].indirect(cols), weight[c][:, j0:j1], MULT)
+        rows = pool.tile([P, 64], F32, name="rows", align_bytes=64)
+        cols = pool.tile([P, 2, 32], F32, name="cols", align_bytes=64)
+        spread = [pool.tile([P, 8, 2, 2, 16], F32, name="spread%d" % k, align_bytes=64) for k in range(PICKS)]
+        nc.sync.dma_start(rows[:], wgt[0:P:16, :].rearrange("g (a c) -> g a c", c=64))
+        for u in range(2):
+            nc.vector.transpose(cols[:, u, :], rows[:, 32 * u : 32 * u + 32])
+        for k in range(PICKS):
+            src = cols[:].rearrange("p u (g a) -> p a u g", g=2)[:, 8 * k : 8 * k + 8, :, :].unsqueeze(4).to_broadcast([P, 8, 2, 2, 16])
+            if k == 0:
+                nc.vector.tensor_copy(spread[k][:], src)
+            else:
+                nc.scalar.copy(spread[k][:], src)
+        for k in range(PICKS):
+            nc.vector.transpose(weight[k][:], spread[k][:].rearrange("p a u g r -> p (a u g r)"))
 
-        def interleave(on_scalar, dst, src):
-            dst = dst.rearrange("p (g i) t -> p g t i", i=RUN)
-            src = src.rearrange("p t (g i) -> p g t i", i=RUN)
+        def load_plane(t):
+            nc.sync.dma_start(plane[t][:], x_rows[:, t, :])
+
+        def load_scales():
+            for q in range(4):
+                nc.sync.dma_start(
+                    w4_scale[:].bitcast(I32)[32 * q : 32 * q + 4, :],
+                    w4_scales[0].bitcast(I32)[4 * q : 4 * q + 4, :],
+                )
+
+        def load_w4():
+            nc.sync.dma_start(w4_codes[:].bitcast(I32), w4_words[0].bitcast(I32))
+
+        def load_wd(u):
+            nc.sync.dma_start(wd_raw[u], wd_rows[:, :, PSTART[u] * P : (PSTART[u] + PARTS[u]) * P])
+
+        def load_bias():
+            with nc.allow_non_contiguous_dma(reason="one bias value to a partition"):
+                nc.sync.dma_start(bias[:], b.rearrange("(m p) -> p m", p=P))
+
+        load_plane(0)
+        nc.sync.dma_start(offsets[:], offs)
+        load_plane(1)
+        load_plane(2)
+        load_scales()
+        load_w4()
+        load_plane(3)
+        load_wd(0)
+        load_wd(1)
+        load_bias()
+
+        def copy(on_scalar, dst, src):
             if on_scalar:
                 nc.scalar.copy(dst, src)
             else:
                 nc.vector.tensor_copy(dst, src)
 
-        def interleave_x(on_scalar, pair, h, c, j0, j1):
-            planes = slice(2 * pair, 2 * pair + 2)
-            dst = x_bf[h][:, c * HALF + j0 : c * HALF + j1, planes]
-            src = picked[c][:, planes, h * HALF + j0 : h * HALF + j1].rearrange("p t w -> p w t")
-            if on_scalar:
-                nc.scalar.copy(dst, src)
-            else:
-                nc.vector.tensor_copy(dst, src)
+        def gather_wide(t, k):
+            nc.vector.tensor_tensor(
+                stage[:, (t * PICKS + k) * J : (t * PICKS + k + 1) * J],
+                plane[t][:].indirect(offsets[:, k * J // 16 : (k + 1) * J // 16]),
+                weight[k][:],
+                MULT,
+            )
+
+        def slot(c, k):
+            return {(0,0):OWN,(0,1):OWN+1,(1,0):OWN+2,(1,1):OWN+3,(2,0):OWN,(2,1):RAW,(3,0):RAW+1,(3,1):RAW+8}[c,k]
+
+        def g(c, k):
+            w = WIDTH[c]
+            j0 = k * J + START[c]
+            nc.vector.tensor_tensor(
+                stage[:, slot(c, k) * W : slot(c, k) * W + w],
+                plane[PACK - 1][:].indirect(offsets[:, j0 // 16 : (j0 + w) // 16]),
+                weight[k][:, START[c] : START[c] + w],
+                MULT,
+            )
+
+        def pair(on_scalar, c, k, first, second, t0):
+            w = WIDTH[c]
+            step = (second - first) * W // w
+            src = stage[:, first * W : first * W + (step + 1) * w].rearrange("p (x w) -> p x w", w=w)[:, 0 : step + 1 : step, :]
+            copy(on_scalar, x_bf[c][:, k * w : (k + 1) * w, t0 : t0 + 2], src.rearrange("p t w -> p w t"))
+
+        def early(c, k):
+            pair(True, c, k, 4 * k + START[c] // W, 8 + 4 * k + START[c] // W, 0)
+
+        def late(on_scalar, c, k):
+            pair(on_scalar, c, k, 16 + 4 * k + START[c] // W, slot(c, k), 2)
 
         def quantize(codes, scale, src, w0, w1):
             nc.vector.quantize_mx(codes[:, w0:w1].bitcast(FP8X4), scale[:, w0:w1], src[:, w0:w1, :].rearrange("p w t -> p (w t)"))
 
-        def pass_w4(h, m):
+        def q(c, k):
+            quantize(x_codes[c], x_scale[c], x_bf[c], k * WIDTH[c], (k + 1) * WIDTH[c])
+
+        def q2(c):
+            quantize(x_codes[c], x_scale[c], x_bf[c], 0, 2 * W)
+
+        def iw(u, on_scalar=True):
+            copy(on_scalar, wd_bf[u][:].rearrange("p (g i) t -> p g t i", i=RUN), wd_raw[u].rearrange("p t (g i) -> p g t i", i=RUN))
+
+        def qw(u):
+            quantize(wd_codes[u], wd_scale[u], wd_bf[u], 0, PARTS[u] * P)
+
+        def pass_w4(dst, m, c, w0, w1, start, stop):
             nc.tensor.matmul_mx(
-                acc[h, m][:],
+                dst,
                 lhsT=w4_codes[:, 2 * P * m : 2 * P * (m + 1)].bitcast(FP4X4),
                 lhsT_scale=w4_scale[:, P * m : P * (m + 1)],
-                rhs=x_codes[h][:].bitcast(FP8X4),
-                rhs_scale=x_scale[h][:],
-                start=True,
-                stop=False,
+                rhs=x_codes[c][:, w0:w1].bitcast(FP8X4),
+                rhs_scale=x_scale[c][:, w0:w1],
+                start=start,
+                stop=stop,
             )
 
-        def pass_wd(h, m):
-            u, cols = m // 2, slice(P * (m % 2), P * (m % 2 + 1))
+        def pass_wd(dst, m, c, w0, w1, start, stop):
+            u = [v for v in range(len(PARTS)) if PSTART[v] <= m][-1]
+            mc = slice(P * (m - PSTART[u]), P * (m - PSTART[u] + 1))
             nc.tensor.matmul_mx(
-                acc[h, m][:],
-                lhsT=wd_codes[u][:, cols].bitcast(FP8X4),
-                lhsT_scale=wd_scale[u][:, cols],
-                rhs=x_codes[h][:].bitcast(FP8X4),
-                rhs_scale=x_scale[h][:],
-                start=False,
+                dst,
+                lhsT=wd_codes[u][:, mc].bitcast(FP8X4),
+                lhsT_scale=wd_scale[u][:, mc],
+                rhs=x_codes[c][:, w0:w1].bitcast(FP8X4),
+                rhs_scale=x_scale[c][:, w0:w1],
+                start=start,
+                stop=stop,
+            )
+
+        def warmup(dst, n):
+            nc.tensor.matmul_mx(
+                dst[:, 0:n],
+                lhsT=wd_codes[0][:, 0:P].bitcast(FP8X4),
+                lhsT_scale=wd_scale[0][:, 0:P],
+                rhs=w4_codes[:, 0 : 2 * n].bitcast(FP4X4),
+                rhs_scale=w4_scale[:, 0:n],
+                start=True,
                 stop=True,
             )
 
-        def finish(h, m, on_scalar, j0, j1):
-            w = j1 - j0
-            first = pool.tile([P, w], F32, name="first%d_%d_%d" % (h, m, j0))
-            prod = pool.tile([P, w], F32, name="prod%d_%d_%d" % (h, m, j0))
-            res = pool.tile([P, w], F32, name="res%d_%d_%d" % (h, m, j0))
-            if on_scalar:
-                nc.scalar.copy(first[:], acc[h, m][:, j0:j1])
-            else:
-                nc.vector.tensor_copy(first[:], acc[h, m][:, j0:j1])
-            nc.vector.tensor_tensor(prod[:], acc[h, m][:, HALF + j0 : HALF + j1], first[:], MULT)
-            nc.scalar.activation(res[:], prod[:], GELU, bias=bias[:, m : m + 1])
-            nc.sync.dma_start(out[P * m : P * (m + 1), h * HALF + j0 : h * HALF + j1], res[:])
+        def mm(c, h):
+            for i in range(2):
+                m, o = 2 * h + i, 2 * W * i
+                pass_w4(bank[c, h][:, o : o + W], m, c, 0, W, True, False)
+                pass_w4(bank[c, h][:, o + W : o + 2 * W], m, c, W, 2 * W, False, False)
+                pass_wd(bank[c, h][:, o : o + 2 * W], m, c, 0, 2 * W, False, True)
+
+        def mm4(c, h):
+            for i in range(2):
+                for k in range(PICKS):
+                    o = 2 * W * i + W * k
+                    pass_w4(bank[c, h][:, o : o + W], 2 * h + i, c, k * W, (k + 1) * W, i == 0 and k == 0, False)
+
+        def mmd(c, h):
+            for i in range(2):
+                pass_wd(bank[c, h][:, 2 * W * i : 2 * W * (i + 1)], 2 * h + i, c, 0, 2 * W, False, i == 1)
+
+        def big4(c, m):
+            pass_w4(bank[c, m][:], m, c, 0, 2 * HALF, True, False)
+
+        def bigd(c, m):
+            pass_wd(bank[c, m][:], m, c, 0, 2 * HALF, False, True)
+
+        def mmd1(c, h, i):
+            pass_wd(bank[c, h][:, 2 * W * i : 2 * W * (i + 1)], 2 * h + i, c, 0, 2 * W, False, i == 1)
+
+        def warmx(dst, n):
+            for i in range(n):
+                pass_w4(dst[:, i * W : (i + 1) * W], 0, 0, 0, W, True, True)
+
+        def mm_pick(dst, c, k, ms):
+            for i, m in enumerate(ms):
+                pass_w4(dst[:, i * W : (i + 1) * W], m, c, k * W, (k + 1) * W, True, False)
+                pass_wd(dst[:, i * W : (i + 1) * W], m, c, k * W, (k + 1) * W, False, True)
+
+        first, prod, res = {}, {}, {}
+        for c in range(CHUNKS):
+            for h in range(2 * WIDTH[c] // W):
+                prod[c, h] = pool.tile([P, 2, W], F32, name="prod%d_%d" % (c, h))
+                res[c, h] = pool.tile([P, 2, W], F32, name="res%d_%d" % (c, h))
+                if c < CHUNKS - 1:
+                    tile = pool.tile([P, 2, W], F32, name="first%d_%d" % (c, h))
+                    first[c, h] = tile[:]
+        first[0, 0] = blocks[:, RAW + 10 : RAW + 12, :]
+        first[1, 0] = blocks[:, RAW + 12 : RAW + 14, :]
+        first_last = pool.tile([P, 4, W], F32, name="first_last")
+
+        def sides(c, h):
+            if WIDTH[c] == HALF:
+                return bank[c, h][:].rearrange("p (k i w) -> p i k w", i=2, k=PICKS)
+            return bank[c, h][:].rearrange("p (i k w) -> p i k w", i=2, k=PICKS)
+
+        def cp(c, h, on_scalar=True):
+            copy(on_scalar, first[c, h], sides(c, h)[:, :, 0, :])
+
+        def pr(c, h):
+            nc.vector.tensor_tensor(prod[c, h][:], sides(c, h)[:, :, 1, :], first[c, h], MULT)
+
+        def red(c, h):
+            nc.vector.tensor_reduce(prod[c, h][:], sides(c, h).rearrange("p i k w -> p i w k"), AX, MULT)
+
+        def act(c, h):
+            if WIDTH[c] == HALF:
+                nc.scalar.activation(res[c, h][:].rearrange("p i w -> p (i w)"), prod[c, h][:].rearrange("p i w -> p (i w)"), GELU, bias=bias[:, h : h + 1])
+                return
+            for i in range(2):
+                m = 2 * h + i
+                nc.scalar.activation(res[c, h][:, i, :], prod[c, h][:, i, :], GELU, bias=bias[:, m : m + 1])
+
+        def store(c, h, eng=nc.sync):
+            if WIDTH[c] == HALF:
+                eng.dma_start(out_rows[:, h, START[c] : START[c] + HALF], res[c, h][:].rearrange("p i w -> p (i w)"))
+                return
+            eng.dma_start(out_rows[:, 2 * h : 2 * h + 2, START[c] : START[c] + W], res[c, h][:])
+
+        def fin(c, h):
+            act(c, h)
+            store(c, h)
+
+        L = CHUNKS - 1
+
+        def last_a0():
+            mm_pick(bank[L, 0], L, 0, range(4))
+
+        def last_cp(on_scalar=True):
+            copy(on_scalar, first_last[:].rearrange("p m w -> p (m w)"), bank[L, 0][:])
+
+        def last_a1(h):
+            if h == 1:
+                bank[L, 2] = psum.tile([P, 4 * W], F32, name="bank0_0")
+            mm_pick(bank[L, 1 + h], L, 1, (2 * h, 2 * h + 1))
+
+        def last_pr(h):
+            nc.vector.tensor_tensor(
+                prod[L, h][:], bank[L, 1 + h][:, 0 : 2 * W].rearrange("p (i w) -> p i w", i=2), first_last[:, 2 * h : 2 * h + 2, :], MULT
+            )
 
         for t in range(PACK - 1):
-            for c in range(PICKS):
-                gather(t, c, 0, J)
-                if t == 1:
-                    for h in range(2):
-                        interleave_x(True, 0, h, c, 0, HALF)
-        last = PACK - 1
-        Q = HALF // 2
-        for j0 in (0, Q):
-            gather(last, 0, j0, j0 + Q)
-            interleave_x(True, 1, 0, 0, j0, j0 + Q)
-        for j0 in (0, Q):
-            gather(last, 1, j0, j0 + Q)
-        quantize(x_codes[0], x_scale[0], x_bf[0], 0, Q)
-        for i in range(4):
-            nc.tensor.matmul_mx(
-                acc[1, 3][:, P * (i % 4) : P * (i % 4 + 1)],
-                lhsT=w4_codes[:, 0 : 2 * P].bitcast(FP4X4),
-                lhsT_scale=w4_scale[:, 0:P],
-                rhs=x_codes[0][:, 0:Q].bitcast(FP8X4),
-                rhs_scale=x_scale[0][:, 0:Q],
-                start=True,
-                stop=True,
-            )
-        for j0 in (0, Q):
-            interleave_x(False, 1, 0, 1, j0, j0 + Q)
-        for w0 in (HALF, Q, HALF + Q):
-            quantize(x_codes[0], x_scale[0], x_bf[0], w0, w0 + Q)
-        interleave(True, wd_bf[0][:], wd_raw[0][:])
-        gather(last, 0, HALF, J)
-        quantize(wd_codes[0], wd_scale[0], wd_bf[0], 0, HALF)
-        interleave(True, wd_bf[1][:], wd_raw[1][:])
-        interleave_x(True, 1, 1, 0, 0, HALF)
-        gather(last, 1, HALF, HALF + Q)
-        interleave_x(True, 1, 1, 1, 0, Q)
-        gather(last, 1, HALF + Q, J)
-        quantize(wd_codes[1], wd_scale[1], wd_bf[1], 0, HALF)
-        interleave_x(False, 1, 1, 1, Q, HALF)
-        for w0, w1 in ((0, HALF), (HALF, HALF + Q), (HALF + Q, 2 * HALF)):
-            quantize(x_codes[1], x_scale[1], x_bf[1], w0, w1)
+            for k in range(PICKS):
+                gather_wide(t, k)
+            if t == 1:
+                for k in range(PICKS):
+                    for c in range(CHUNKS):
+                        early(c, k)
+        iw(0, False)
+        qw(0)
+        iw(1)
+        qw(1)
+        pieces = [(c, k) for c in range(CHUNKS) for k in range(PICKS)]
+        for s, (c, k) in enumerate(pieces):
+            g(c, k)
+            late((c, k) != (L, 1), c, k)
+            if s >= 2:
+                q(*pieces[s - 2])
+        for c, k in pieces[len(pieces) - 2 :]:
+            q(c, k)
+        units = sorted([(c, h) for c in range(L) for h in range(2)] + [(L, 0)], key=lambda u: (u[0] + u[1], u[1]))
+        for c, h in units:
+            if c < L:
+                mm4(c, h)
+                mmd(c, h)
+            else:
+                last_a0()
+        for i, (c, h) in enumerate(units):
+            if c == L:
+                last_cp()
+                continue
+            if i < 4:
+                cp(c, h)
+                pr(c, h)
+            else:
+                red(c, h)
+            if i == 0:
+                last_a1(0)
+                last_a1(1)
+            fin(c, h)
         for h in range(2):
-            for m in range(4):
-                pass_w4(h, m)
-                pass_wd(h, m)
-        for h in range(2):
-            for m in range(4):
-                on_scalar = h == 0 or m == 2
-                if (h, m) == (1, 3):
-                    for j0 in (0, Q):
-                        finish(h, m, on_scalar, j0, j0 + Q)
-                else:
-                    finish(h, m, on_scalar, 0, HALF)
+            last_pr(h)
+            fin(L, h)

@@ -14,7 +14,7 @@ U8 = mybir.dt.uint8
 FP8X4 = mybir.dt.float8_e4m3fn_x4
 FP4X4 = mybir.dt.float4_e2m1fn_x4
 MULT = mybir.AluOpType.mult
-AX = mybir.AxisListType.X
+INNER = mybir.AxisListType.X
 GELU = mybir.ActivationFunctionType.Gelu_apprx_tanh
 
 P = 128
@@ -23,11 +23,7 @@ PICKS = 2
 HALF = 256
 RUN = 4
 W = 128
-WIDTH = [128] * 4
-START = [sum(WIDTH[:c]) for c in range(len(WIDTH))]
-CHUNKS = len(WIDTH)
-PARTS = [2, 2]
-PSTART = [sum(PARTS[:u]) for u in range(len(PARTS))]
+PIECES = [(0, 0, W), (1, 0, W), (0, W, W), (1, W, W), (0, 2 * W, W), (0, 3 * W, W), (1, 2 * W, W), (1, 3 * W, W)]
 
 
 def tile_list_dl_prod_gelu_kernel(tc, xT, wgt, w4_words, w4_scales, wd, b, offs, out):
@@ -37,30 +33,33 @@ def tile_list_dl_prod_gelu_kernel(tc, xT, wgt, w4_words, w4_scales, wd, b, offs,
         psum = ctx.enter_context(tc.psum_pool(name="psum", bufs=1))
 
         offsets = pool.tile([P, PICKS * J // 16], U16, name="offsets")
-        weight = [pool.tile([P, J], F32, name="weight%d" % k, align_bytes=64) for k in range(PICKS)]
+        weights = pool.tile([P, PICKS * J], F32, name="weights", align_bytes=64)
         plane = [pool.tile([P, T], F32, name="plane%d" % t) for t in range(PACK)]
         w4_codes = pool.tile([P, 2 * N], U8, name="w4_codes", align_bytes=64)
         w4_scale = pool.tile([P, N], U8, name="w4_scale", align_bytes=64)
         bias = pool.tile([P, N // P], F32, name="bias")
-        OWN = 3 * 8
-        RAW = OWN + 8
-        stage = pool.tile([P, (RAW + 16) * W], F32, name="stage")
-        blocks = stage[:].rearrange("p (x w) -> p x w", w=W)
-        wd_raw = [stage[:, (RAW + 4 * PSTART[u]) * W : (RAW + 4 * (PSTART[u] + n)) * W].rearrange("p (t n) -> p t n", t=PACK) for u, n in enumerate(PARTS)]
-        wd_bf = [pool.tile([P, n * P, PACK], BF16, name="wd_bf%d" % u, align_bytes=64) for u, n in enumerate(PARTS)]
-        wd_codes = [pool.tile([P, n * P], U32, name="wd_codes%d" % u, align_bytes=64) for u, n in enumerate(PARTS)]
-        wd_scale = [pool.tile([P, n * P], U8, name="wd_scale%d" % u, align_bytes=64) for u, n in enumerate(PARTS)]
-        x_bf = [pool.tile([P, PICKS * WIDTH[c], PACK], BF16, name="x_bf%d" % c, align_bytes=64) for c in range(CHUNKS)]
-        x_codes = [pool.tile([P, PICKS * WIDTH[c]], U32, name="x_codes%d" % c, align_bytes=64) for c in range(CHUNKS)]
-        x_scale = [pool.tile([P, PICKS * WIDTH[c]], U8, name="x_scale%d" % c, align_bytes=64) for c in range(CHUNKS)]
-        bank = {}
-        for c in range(CHUNKS):
-            for h in range(2 * WIDTH[c] // W):
-                bank[c, h] = psum.tile([P, 4 * W], F32, name="bank%d_%d" % (c, h))
+        OWN = 3 * PICKS * J
+        RAW = OWN + PICKS * J
+        stage = pool.tile([P, RAW + 2 * PACK * HALF + 0], F32, name="stage")
+        wd_raw = [stage[:, RAW + u * PACK * HALF : RAW + (u + 1) * PACK * HALF].rearrange("p (t n) -> p t n", t=PACK) for u in range(2)]
+        wd_bf = [pool.tile([P, HALF, PACK], BF16, name="wd_bf%d" % u, align_bytes=64) for u in range(2)]
+        wd_codes = [pool.tile([P, HALF], U32, name="wd_codes%d" % u, align_bytes=64) for u in range(2)]
+        wd_scale = [pool.tile([P, HALF], U8, name="wd_scale%d" % u, align_bytes=64) for u in range(2)]
+        x_bf = [pool.tile([P, J, PACK], BF16, name="x_bf%d" % v, align_bytes=64) for v in range(2)]
+        x_codes = [pool.tile([P, J], U32, name="x_codes%d" % v, align_bytes=64) for v in range(2)]
+        x_scale = [pool.tile([P, J], U8, name="x_scale%d" % v, align_bytes=64) for v in range(2)]
+        both = [psum.tile([P, J], F32, name="bank%d" % m) for m in range(4)]
+        low = [psum.tile([P, J], F32, name="low%d" % h) for h in range(2)]
+        high = [psum.tile([P, J], F32, name="high%d" % m) for m in range(2)]
+        slot = [OWN, OWN + W, OWN + 2 * W, OWN + 3 * W, OWN, RAW, RAW + W, RAW + 8 * W]
 
         x_rows = xT.rearrange("(p t) c -> p t c", t=PACK)
         wd_rows = wd.rearrange("(p t) n -> p t n", t=PACK)
-        out_rows = out.rearrange("(m p) j -> p m j", p=P)
+
+        rows = pool.tile([P, 64], F32, name="rows", align_bytes=64)
+        cols = pool.tile([P, 2, 32], F32, name="cols", align_bytes=64)
+        spread = [pool.tile([P, 8, 2, 2, 16], F32, name="spread%d" % k, align_bytes=64) for k in range(PICKS)]
+        nc.sync.dma_start(rows[:], wgt[0:P:16, :].rearrange("g (a c) -> g a c", c=64))
 
         nc.vector.memset(w4_scale[:].bitcast(I32), 0)
         zero = pool.tile([P, 1], F32, name="zero")
@@ -68,27 +67,26 @@ def tile_list_dl_prod_gelu_kernel(tc, xT, wgt, w4_words, w4_scales, wd, b, offs,
         nc.vector.memset(zero[:], 0.0)
         nc.scalar.activation(warm[:], zero[:], GELU)
 
-        rows = pool.tile([P, 64], F32, name="rows", align_bytes=64)
-        cols = pool.tile([P, 2, 32], F32, name="cols", align_bytes=64)
-        spread = [pool.tile([P, 8, 2, 2, 16], F32, name="spread%d" % k, align_bytes=64) for k in range(PICKS)]
-        nc.sync.dma_start(rows[:], wgt[0:P:16, :].rearrange("g (a c) -> g a c", c=64))
+        def copy(on_scalar, dst, src):
+            if on_scalar:
+                nc.scalar.copy(dst, src)
+            else:
+                nc.vector.tensor_copy(dst, src)
+
         for u in range(2):
             nc.vector.transpose(cols[:, u, :], rows[:, 32 * u : 32 * u + 32])
         for k in range(PICKS):
             src = cols[:].rearrange("p u (g a) -> p a u g", g=2)[:, 8 * k : 8 * k + 8, :, :].unsqueeze(4).to_broadcast([P, 8, 2, 2, 16])
-            if k == 0:
-                nc.vector.tensor_copy(spread[k][:], src)
-            else:
-                nc.scalar.copy(spread[k][:], src)
+            copy(k == 1, spread[k][:], src)
         for k in range(PICKS):
-            nc.vector.transpose(weight[k][:], spread[k][:].rearrange("p a u g r -> p (a u g r)"))
+            nc.vector.transpose(weights[:, k * J : (k + 1) * J], spread[k][:].rearrange("p a u g r -> p (a u g r)"))
 
         def load_plane(t):
             nc.sync.dma_start(plane[t][:], x_rows[:, t, :])
 
-        def load_scales():
+        def load_scales(eng=nc.sync):
             for q in range(4):
-                nc.sync.dma_start(
+                eng.dma_start(
                     w4_scale[:].bitcast(I32)[32 * q : 32 * q + 4, :],
                     w4_scales[0].bitcast(I32)[4 * q : 4 * q + 4, :],
                 )
@@ -97,11 +95,11 @@ def tile_list_dl_prod_gelu_kernel(tc, xT, wgt, w4_words, w4_scales, wd, b, offs,
             nc.sync.dma_start(w4_codes[:].bitcast(I32), w4_words[0].bitcast(I32))
 
         def load_wd(u):
-            nc.sync.dma_start(wd_raw[u], wd_rows[:, :, PSTART[u] * P : (PSTART[u] + PARTS[u]) * P])
+            nc.sync.dma_start(wd_raw[u], wd_rows[:, :, u * HALF : (u + 1) * HALF])
 
-        def load_bias():
+        def load_bias(eng=nc.sync):
             with nc.allow_non_contiguous_dma(reason="one bias value to a partition"):
-                nc.sync.dma_start(bias[:], b.rearrange("(m p) -> p m", p=P))
+                eng.dma_start(bias[:], b.rearrange("(m p) -> p m", p=P))
 
         load_plane(0)
         nc.sync.dma_start(offsets[:], offs)
@@ -114,231 +112,145 @@ def tile_list_dl_prod_gelu_kernel(tc, xT, wgt, w4_words, w4_scales, wd, b, offs,
         load_wd(1)
         load_bias()
 
-        def copy(on_scalar, dst, src):
-            if on_scalar:
-                nc.scalar.copy(dst, src)
-            else:
-                nc.vector.tensor_copy(dst, src)
+        def gather(t, at, e0, n):
+            nc.vector.tensor_tensor(stage[:, at : at + n], plane[t][:].indirect(offsets[:, e0 // 16 : (e0 + n) // 16]), weights[:, e0 : e0 + n], MULT)
 
-        def gather_wide(t, k):
-            nc.vector.tensor_tensor(
-                stage[:, (t * PICKS + k) * J : (t * PICKS + k + 1) * J],
-                plane[t][:].indirect(offsets[:, k * J // 16 : (k + 1) * J // 16]),
-                weight[k][:],
-                MULT,
-            )
+        def where(s):
+            k, j0, w = PIECES[s]
+            return j0 // HALF, k * HALF + j0 % HALF, w
 
-        def slot(c, k):
-            return {(0,0):OWN,(0,1):OWN+1,(1,0):OWN+2,(1,1):OWN+3,(2,0):OWN,(2,1):RAW,(3,0):RAW+1,(3,1):RAW+8}[c,k]
+        def pair(on_scalar, v, c0, w, first, second, t0):
+            step = (second - first) // w
+            src = stage[:, first : first + (step + 1) * w].rearrange("p (x w) -> p x w", w=w)[:, 0 : step + 1 : step, :]
+            copy(on_scalar, x_bf[v][:, c0 : c0 + w, t0 : t0 + 2], src.rearrange("p t w -> p w t"))
 
-        def g(c, k):
-            w = WIDTH[c]
-            j0 = k * J + START[c]
-            nc.vector.tensor_tensor(
-                stage[:, slot(c, k) * W : slot(c, k) * W + w],
-                plane[PACK - 1][:].indirect(offsets[:, j0 // 16 : (j0 + w) // 16]),
-                weight[k][:, START[c] : START[c] + w],
-                MULT,
-            )
+        def early(s):
+            k, j0, w = PIECES[s]
+            v, c0, w = where(s)
+            pair(True, v, c0, w, k * J + j0, PICKS * J + k * J + j0, 0)
 
-        def pair(on_scalar, c, k, first, second, t0):
-            w = WIDTH[c]
-            step = (second - first) * W // w
-            src = stage[:, first * W : first * W + (step + 1) * w].rearrange("p (x w) -> p x w", w=w)[:, 0 : step + 1 : step, :]
-            copy(on_scalar, x_bf[c][:, k * w : (k + 1) * w, t0 : t0 + 2], src.rearrange("p t w -> p w t"))
+        def g(s):
+            k, j0, w = PIECES[s]
+            gather(PACK - 1, slot[s], k * J + j0, w)
 
-        def early(c, k):
-            pair(True, c, k, 4 * k + START[c] // W, 8 + 4 * k + START[c] // W, 0)
-
-        def late(on_scalar, c, k):
-            pair(on_scalar, c, k, 16 + 4 * k + START[c] // W, slot(c, k), 2)
+        def late(s, on_scalar):
+            k, j0, w = PIECES[s]
+            v, c0, w = where(s)
+            pair(on_scalar, v, c0, w, 2 * PICKS * J + k * J + j0, slot[s], 2)
 
         def quantize(codes, scale, src, w0, w1):
             nc.vector.quantize_mx(codes[:, w0:w1].bitcast(FP8X4), scale[:, w0:w1], src[:, w0:w1, :].rearrange("p w t -> p (w t)"))
 
-        def q(c, k):
-            quantize(x_codes[c], x_scale[c], x_bf[c], k * WIDTH[c], (k + 1) * WIDTH[c])
+        def q(s):
+            v, c0, w = where(s)
+            quantize(x_codes[v], x_scale[v], x_bf[v], c0, c0 + w)
 
-        def q2(c):
-            quantize(x_codes[c], x_scale[c], x_bf[c], 0, 2 * W)
-
-        def iw(u, on_scalar=True):
+        def iw(u, on_scalar):
             copy(on_scalar, wd_bf[u][:].rearrange("p (g i) t -> p g t i", i=RUN), wd_raw[u].rearrange("p t (g i) -> p g t i", i=RUN))
 
         def qw(u):
-            quantize(wd_codes[u], wd_scale[u], wd_bf[u], 0, PARTS[u] * P)
+            quantize(wd_codes[u], wd_scale[u], wd_bf[u], 0, HALF)
 
-        def pass_w4(dst, m, c, w0, w1, start, stop):
+        def pass_w4(dst, m, v, w0, w1, start):
             nc.tensor.matmul_mx(
                 dst,
                 lhsT=w4_codes[:, 2 * P * m : 2 * P * (m + 1)].bitcast(FP4X4),
                 lhsT_scale=w4_scale[:, P * m : P * (m + 1)],
-                rhs=x_codes[c][:, w0:w1].bitcast(FP8X4),
-                rhs_scale=x_scale[c][:, w0:w1],
+                rhs=x_codes[v][:, w0:w1].bitcast(FP8X4),
+                rhs_scale=x_scale[v][:, w0:w1],
                 start=start,
-                stop=stop,
+                stop=False,
             )
 
-        def pass_wd(dst, m, c, w0, w1, start, stop):
-            u = [v for v in range(len(PARTS)) if PSTART[v] <= m][-1]
-            mc = slice(P * (m - PSTART[u]), P * (m - PSTART[u] + 1))
+        def pass_wd(dst, m, v, w0, w1):
+            u, mc = m // 2, slice(P * (m % 2), P * (m % 2 + 1))
             nc.tensor.matmul_mx(
                 dst,
                 lhsT=wd_codes[u][:, mc].bitcast(FP8X4),
                 lhsT_scale=wd_scale[u][:, mc],
-                rhs=x_codes[c][:, w0:w1].bitcast(FP8X4),
-                rhs_scale=x_scale[c][:, w0:w1],
-                start=start,
-                stop=stop,
-            )
-
-        def warmup(dst, n):
-            nc.tensor.matmul_mx(
-                dst[:, 0:n],
-                lhsT=wd_codes[0][:, 0:P].bitcast(FP8X4),
-                lhsT_scale=wd_scale[0][:, 0:P],
-                rhs=w4_codes[:, 0 : 2 * n].bitcast(FP4X4),
-                rhs_scale=w4_scale[:, 0:n],
-                start=True,
+                rhs=x_codes[v][:, w0:w1].bitcast(FP8X4),
+                rhs_scale=x_scale[v][:, w0:w1],
+                start=False,
                 stop=True,
             )
 
-        def mm(c, h):
-            for i in range(2):
-                m, o = 2 * h + i, 2 * W * i
-                pass_w4(bank[c, h][:, o : o + W], m, c, 0, W, True, False)
-                pass_w4(bank[c, h][:, o + W : o + 2 * W], m, c, W, 2 * W, False, False)
-                pass_wd(bank[c, h][:, o : o + 2 * W], m, c, 0, 2 * W, False, True)
+        def both_mm(m):
+            for i, c0 in enumerate((0, HALF, W, HALF + W)):
+                pass_w4(both[m][:, c0 : c0 + W], m, 0, c0, c0 + W, i == 0)
+            pass_wd(both[m][:], m, 0, 0, J)
 
-        def mm4(c, h):
-            for i in range(2):
-                for k in range(PICKS):
-                    o = 2 * W * i + W * k
-                    pass_w4(bank[c, h][:, o : o + W], 2 * h + i, c, k * W, (k + 1) * W, i == 0 and k == 0, False)
+        def one_pick(dst, m, k):
+            for e in range(2):
+                pass_w4(dst[:, e * W : (e + 1) * W], m, 1, k * HALF + e * W, k * HALF + (e + 1) * W, e == 0)
+            pass_wd(dst, m, 1, k * HALF, (k + 1) * HALF)
 
-        def mmd(c, h):
-            for i in range(2):
-                pass_wd(bank[c, h][:, 2 * W * i : 2 * W * (i + 1)], 2 * h + i, c, 0, 2 * W, False, i == 1)
+        def low_mm(m):
+            one_pick(low[m // 2][:, (m % 2) * HALF : (m % 2 + 1) * HALF], m, 0)
 
-        def big4(c, m):
-            pass_w4(bank[c, m][:], m, c, 0, 2 * HALF, True, False)
+        def high_mm(m):
+            if m >= 2:
+                high.append(psum.tile([P, J], F32, name="bank%d" % (m - 2)))
+            one_pick(high[m][:, 0:HALF], m, 1)
 
-        def bigd(c, m):
-            pass_wd(bank[c, m][:], m, c, 0, 2 * HALF, False, True)
+        prod = {(v, m): pool.tile([P, HALF], F32, name="prod%d_%d" % (v, m)) for v in range(2) for m in range(4)}
+        res = {(v, m): pool.tile([P, HALF], F32, name="res%d_%d" % (v, m)) for v in range(2) for m in range(4)}
+        first = [RAW + 10 * W, RAW + 12 * W, OWN + 4 * W, OWN + 6 * W]
+        first_low = [pool.tile([P, J], F32, name="first_low%d" % h) for h in range(2)]
 
-        def mmd1(c, h, i):
-            pass_wd(bank[c, h][:, 2 * W * i : 2 * W * (i + 1)], 2 * h + i, c, 0, 2 * W, False, i == 1)
+        def cp(m, on_scalar=True):
+            copy(on_scalar, stage[:, first[m] : first[m] + HALF], both[m][:, 0:HALF])
 
-        def warmx(dst, n):
-            for i in range(n):
-                pass_w4(dst[:, i * W : (i + 1) * W], 0, 0, 0, W, True, True)
+        def pr(m):
+            nc.vector.tensor_tensor(prod[0, m][:], both[m][:, HALF:J], stage[:, first[m] : first[m] + HALF], MULT)
 
-        def mm_pick(dst, c, k, ms):
-            for i, m in enumerate(ms):
-                pass_w4(dst[:, i * W : (i + 1) * W], m, c, k * W, (k + 1) * W, True, False)
-                pass_wd(dst[:, i * W : (i + 1) * W], m, c, k * W, (k + 1) * W, False, True)
+        def red(m):
+            nc.vector.tensor_reduce(prod[0, m][:], both[m][:].rearrange("p (k w) -> p w k", k=PICKS), INNER, MULT)
 
-        first, prod, res = {}, {}, {}
-        for c in range(CHUNKS):
-            for h in range(2 * WIDTH[c] // W):
-                prod[c, h] = pool.tile([P, 2, W], F32, name="prod%d_%d" % (c, h))
-                res[c, h] = pool.tile([P, 2, W], F32, name="res%d_%d" % (c, h))
-                if c < CHUNKS - 1:
-                    tile = pool.tile([P, 2, W], F32, name="first%d_%d" % (c, h))
-                    first[c, h] = tile[:]
-        first[0, 0] = blocks[:, RAW + 10 : RAW + 12, :]
-        first[1, 0] = blocks[:, RAW + 12 : RAW + 14, :]
-        first_last = pool.tile([P, 4, W], F32, name="first_last")
+        def low_cp(h, on_scalar):
+            copy(on_scalar, first_low[h][:], low[h][:])
 
-        def sides(c, h):
-            if WIDTH[c] == HALF:
-                return bank[c, h][:].rearrange("p (k i w) -> p i k w", i=2, k=PICKS)
-            return bank[c, h][:].rearrange("p (i k w) -> p i k w", i=2, k=PICKS)
+        def high_pr(m, j0=0, j1=HALF):
+            nc.vector.tensor_tensor(prod[1, m][:, j0:j1], high[m][:, j0:j1], first_low[m // 2][:, (m % 2) * HALF + j0 : (m % 2) * HALF + j1], MULT)
 
-        def cp(c, h, on_scalar=True):
-            copy(on_scalar, first[c, h], sides(c, h)[:, :, 0, :])
+        def fin(v, m, j0=0, j1=HALF):
+            nc.scalar.activation(res[v, m][:, j0:j1], prod[v, m][:, j0:j1], GELU, bias=bias[:, m : m + 1])
+            nc.sync.dma_start(out[P * m : P * (m + 1), v * HALF + j0 : v * HALF + j1], res[v, m][:, j0:j1])
 
-        def pr(c, h):
-            nc.vector.tensor_tensor(prod[c, h][:], sides(c, h)[:, :, 1, :], first[c, h], MULT)
+        gather(0, 0, 0, PICKS * J)
+        for k in range(PICKS):
+            gather(1, PICKS * J + k * J, k * J, J)
+        for k in range(PICKS):
+            for s in range(len(PIECES)):
+                if PIECES[s][0] == k:
+                    early(s)
+        gather(2, 2 * PICKS * J, 0, PICKS * J)
 
-        def red(c, h):
-            nc.vector.tensor_reduce(prod[c, h][:], sides(c, h).rearrange("p i k w -> p i w k"), AX, MULT)
-
-        def act(c, h):
-            if WIDTH[c] == HALF:
-                nc.scalar.activation(res[c, h][:].rearrange("p i w -> p (i w)"), prod[c, h][:].rearrange("p i w -> p (i w)"), GELU, bias=bias[:, h : h + 1])
-                return
-            for i in range(2):
-                m = 2 * h + i
-                nc.scalar.activation(res[c, h][:, i, :], prod[c, h][:, i, :], GELU, bias=bias[:, m : m + 1])
-
-        def store(c, h, eng=nc.sync):
-            if WIDTH[c] == HALF:
-                eng.dma_start(out_rows[:, h, START[c] : START[c] + HALF], res[c, h][:].rearrange("p i w -> p (i w)"))
-                return
-            eng.dma_start(out_rows[:, 2 * h : 2 * h + 2, START[c] : START[c] + W], res[c, h][:])
-
-        def fin(c, h):
-            act(c, h)
-            store(c, h)
-
-        L = CHUNKS - 1
-
-        def last_a0():
-            mm_pick(bank[L, 0], L, 0, range(4))
-
-        def last_cp(on_scalar=True):
-            copy(on_scalar, first_last[:].rearrange("p m w -> p (m w)"), bank[L, 0][:])
-
-        def last_a1(h):
-            if h == 1:
-                bank[L, 2] = psum.tile([P, 4 * W], F32, name="bank0_0")
-            mm_pick(bank[L, 1 + h], L, 1, (2 * h, 2 * h + 1))
-
-        def last_pr(h):
-            nc.vector.tensor_tensor(
-                prod[L, h][:], bank[L, 1 + h][:, 0 : 2 * W].rearrange("p (i w) -> p i w", i=2), first_last[:, 2 * h : 2 * h + 2, :], MULT
-            )
-
-        for t in range(PACK - 1):
-            for k in range(PICKS):
-                gather_wide(t, k)
-            if t == 1:
-                for k in range(PICKS):
-                    for c in range(CHUNKS):
-                        early(c, k)
-        iw(0, False)
-        qw(0)
-        iw(1)
-        qw(1)
-        pieces = [(c, k) for c in range(CHUNKS) for k in range(PICKS)]
-        for s, (c, k) in enumerate(pieces):
-            g(c, k)
-            late((c, k) != (L, 1), c, k)
+        for u in range(2):
+            iw(u, u == 1)
+            qw(u)
+        for s in range(len(PIECES)):
+            g(s)
+            late(s, s < 7)
             if s >= 2:
-                q(*pieces[s - 2])
-        for c, k in pieces[len(pieces) - 2 :]:
-            q(c, k)
-        units = sorted([(c, h) for c in range(L) for h in range(2)] + [(L, 0)], key=lambda u: (u[0] + u[1], u[1]))
-        for c, h in units:
-            if c < L:
-                mm4(c, h)
-                mmd(c, h)
+                q(s - 2)
+        for s in range(len(PIECES) - 2, len(PIECES)):
+            q(s)
+        for m in range(4):
+            both_mm(m)
+        for m in range(4):
+            low_mm(m)
+        for m in range(4):
+            if m < 3:
+                cp(m)
+                pr(m)
             else:
-                last_a0()
-        for i, (c, h) in enumerate(units):
-            if c == L:
-                last_cp()
-                continue
-            if i < 4:
-                cp(c, h)
-                pr(c, h)
-            else:
-                red(c, h)
-            if i == 0:
-                last_a1(0)
-                last_a1(1)
-            fin(c, h)
+                red(m)
+            if m == 1:
+                for i in range(4):
+                    high_mm(i)
+            fin(0, m)
         for h in range(2):
-            last_pr(h)
-            fin(L, h)
+            low_cp(h, h == 0)
+        for m in range(4):
+            high_pr(m)
+            fin(1, m)

@@ -23,6 +23,7 @@ PICKS = 2
 HALF = 256
 RUN = 4
 W = 128
+LATER = W
 PIECES = [(0, 0, W), (1, 0, W), (0, W, W), (1, W, W), (0, 2 * W, W), (0, 3 * W, W), (1, 2 * W, W), (1, 3 * W, W)]
 
 
@@ -136,7 +137,10 @@ def tile_list_dl_prod_gelu_kernel(tc, xT, wgt, w4_words, w4_scales, wd, b, offs,
         def late(s, on_scalar):
             k, j0, w = PIECES[s]
             v, c0, w = where(s)
-            pair(on_scalar, v, c0, w, 2 * PICKS * J + k * J + j0, slot[s], 2)
+            e0 = k * J + j0
+            if e0 >= PICKS * J - LATER:
+                e0 = e0 - (PICKS * J - LATER) + 0
+            pair(on_scalar, v, c0, w, 2 * PICKS * J + e0, slot[s], 2)
 
         def quantize(codes, scale, src, w0, w1):
             nc.vector.quantize_mx(codes[:, w0:w1].bitcast(FP8X4), scale[:, w0:w1], src[:, w0:w1, :].rearrange("p w t -> p (w t)"))
@@ -209,6 +213,10 @@ def tile_list_dl_prod_gelu_kernel(tc, xT, wgt, w4_words, w4_scales, wd, b, offs,
         def low_cp(h, on_scalar):
             copy(on_scalar, first_low[h][:], low[h][:])
 
+        def low_cp1(m, on_scalar):
+            c0 = (m % 2) * HALF
+            copy(on_scalar, first_low[m // 2][:, c0 : c0 + HALF], low[m // 2][:, c0 : c0 + HALF])
+
         def high_pr(m, j0=0, j1=HALF):
             nc.vector.tensor_tensor(prod[1, m][:, j0:j1], high[m][:, j0:j1], first_low[m // 2][:, (m % 2) * HALF + j0 : (m % 2) * HALF + j1], MULT)
 
@@ -216,19 +224,36 @@ def tile_list_dl_prod_gelu_kernel(tc, xT, wgt, w4_words, w4_scales, wd, b, offs,
             nc.scalar.activation(res[v, m][:, j0:j1], prod[v, m][:, j0:j1], GELU, bias=bias[:, m : m + 1])
             nc.sync.dma_start(out[P * m : P * (m + 1), v * HALF + j0 : v * HALF + j1], res[v, m][:, j0:j1])
 
+        wv, wc, ww = where(6)
+        nc.vector.memset(x_bf[wv][:, wc : wc + ww, :].rearrange("p w t -> p (w t)").bitcast(I32), 0)
         gather(0, 0, 0, PICKS * J)
-        for k in range(PICKS):
-            gather(1, PICKS * J + k * J, k * J, J)
+        for e0, n in ((0, HALF), (HALF, HALF), (J, J)):
+            gather(1, PICKS * J + e0, e0, n)
         for k in range(PICKS):
             for s in range(len(PIECES)):
                 if PIECES[s][0] == k:
                     early(s)
-        gather(2, 2 * PICKS * J, 0, PICKS * J)
+        gather(2, 2 * PICKS * J, 0, PICKS * J - LATER)
 
+        warm_codes = pool.tile([P, P], U32, name="warm_codes", align_bytes=64)
+        warm_scale = pool.tile([P, P], U8, name="warm_scale", align_bytes=64)
+        nc.vector.quantize_mx(warm_codes[:].bitcast(FP8X4), warm_scale[:], x_bf[wv][:, wc : wc + ww, :].rearrange("p w t -> p (w t)"))
+        for n in (J, HALF):
+            nc.tensor.matmul_mx(
+                high[1][:, 0:n],
+                lhsT=warm_codes[:].bitcast(FP8X4),
+                lhsT_scale=warm_scale[:],
+                rhs=w4_codes[:, 0 : 2 * n].bitcast(FP4X4),
+                rhs_scale=w4_scale[:, 0:n],
+                start=True,
+                stop=True,
+            )
         for u in range(2):
             iw(u, u == 1)
             qw(u)
         for s in range(len(PIECES)):
+            if s == 7:
+                gather(2, 2 * PICKS * J + 0, PICKS * J - LATER, LATER)
             g(s)
             late(s, s < 7)
             if s >= 2:
@@ -251,6 +276,9 @@ def tile_list_dl_prod_gelu_kernel(tc, xT, wgt, w4_words, w4_scales, wd, b, offs,
             fin(0, m)
         for h in range(2):
             low_cp(h, h == 0)
-        for m in range(4):
+        for m in range(3):
             high_pr(m)
             fin(1, m)
+        for j0 in (0, W):
+            high_pr(3, j0, j0 + W)
+            fin(1, 3, j0, j0 + W)

@@ -1,6 +1,7 @@
 from contextlib import ExitStack
 
 import concourse.mybir as mybir
+from concourse.masks import make_identity
 
 K, N, T, J = 512, 512, 2048, 512
 FLOPS = 2 * 2 * 2 * K * N * J
@@ -23,7 +24,7 @@ PICKS = 2
 HALF = 256
 RUN = 4
 W = 128
-LATER = W
+LATER = 0
 PIECES = [(0, 0, W), (1, 0, W), (0, W, W), (1, W, W), (0, 2 * W, W), (0, 3 * W, W), (1, 2 * W, W), (1, 3 * W, W)]
 
 
@@ -52,7 +53,7 @@ def tile_list_dl_prod_gelu_kernel(tc, xT, wgt, w4_words, w4_scales, wd, b, offs,
         both = [psum.tile([P, J], F32, name="bank%d" % m) for m in range(4)]
         low = [psum.tile([P, J], F32, name="low%d" % h) for h in range(2)]
         high = [psum.tile([P, J], F32, name="high%d" % m) for m in range(2)]
-        slot = [OWN, OWN + W, OWN + 2 * W, OWN + 3 * W, OWN, RAW, RAW + W, RAW + 8 * W]
+        slot = [OWN, OWN + W, OWN + 2 * W, OWN + 3 * W, OWN, RAW, RAW+W, RAW + 8*W]
 
         x_rows = xT.rearrange("(p t) c -> p t c", t=PACK)
         wd_rows = wd.rearrange("(p t) n -> p t n", t=PACK)
@@ -102,11 +103,11 @@ def tile_list_dl_prod_gelu_kernel(tc, xT, wgt, w4_words, w4_scales, wd, b, offs,
             with nc.allow_non_contiguous_dma(reason="one bias value to a partition"):
                 eng.dma_start(bias[:], b.rearrange("(m p) -> p m", p=P))
 
+        load_scales(nc.scalar)
         load_plane(0)
         nc.sync.dma_start(offsets[:], offs)
         load_plane(1)
         load_plane(2)
-        load_scales()
         load_w4()
         load_plane(3)
         load_wd(0)
@@ -138,8 +139,6 @@ def tile_list_dl_prod_gelu_kernel(tc, xT, wgt, w4_words, w4_scales, wd, b, offs,
             k, j0, w = PIECES[s]
             v, c0, w = where(s)
             e0 = k * J + j0
-            if e0 >= PICKS * J - LATER:
-                e0 = e0 - (PICKS * J - LATER) + 0
             pair(on_scalar, v, c0, w, 2 * PICKS * J + e0, slot[s], 2)
 
         def quantize(codes, scale, src, w0, w1):
@@ -224,8 +223,11 @@ def tile_list_dl_prod_gelu_kernel(tc, xT, wgt, w4_words, w4_scales, wd, b, offs,
             nc.scalar.activation(res[v, m][:, j0:j1], prod[v, m][:, j0:j1], GELU, bias=bias[:, m : m + 1])
             nc.sync.dma_start(out[P * m : P * (m + 1), v * HALF + j0 : v * HALF + j1], res[v, m][:, j0:j1])
 
-        wv, wc, ww = where(6)
-        nc.vector.memset(x_bf[wv][:, wc : wc + ww, :].rearrange("p w t -> p (w t)").bitcast(I32), 0)
+        warm_in = pool.tile([P, PACK * P], BF16, name="warm_in", align_bytes=64)
+        warm_codes = pool.tile([P, P], U32, name="warm_codes", align_bytes=64)
+        warm_scale = pool.tile([P, P], U8, name="warm_scale", align_bytes=64)
+        nc.vector.memset(warm_in[:].bitcast(I32), 0)
+        nc.vector.quantize_mx(warm_codes[:].bitcast(FP8X4), warm_scale[:], warm_in[:])
         gather(0, 0, 0, PICKS * J)
         for e0, n in ((0, HALF), (HALF, HALF), (J, J)):
             gather(1, PICKS * J + e0, e0, n)
@@ -234,10 +236,9 @@ def tile_list_dl_prod_gelu_kernel(tc, xT, wgt, w4_words, w4_scales, wd, b, offs,
                 if PIECES[s][0] == k:
                     early(s)
         gather(2, 2 * PICKS * J, 0, PICKS * J - LATER)
-
-        warm_codes = pool.tile([P, P], U32, name="warm_codes", align_bytes=64)
-        warm_scale = pool.tile([P, P], U8, name="warm_scale", align_bytes=64)
-        nc.vector.quantize_mx(warm_codes[:].bitcast(FP8X4), warm_scale[:], x_bf[wv][:, wc : wc + ww, :].rearrange("p w t -> p (w t)"))
+        ident = pool.tile([P, P], F32, name="ident")
+        make_identity(nc, ident[:])
+        nc.tensor.transpose(high[1][:, 0:P], plane[PACK - 1][:, 0:P], ident[:])
         for n in (J, HALF):
             nc.tensor.matmul_mx(
                 high[1][:, 0:n],
@@ -252,8 +253,6 @@ def tile_list_dl_prod_gelu_kernel(tc, xT, wgt, w4_words, w4_scales, wd, b, offs,
             iw(u, u == 1)
             qw(u)
         for s in range(len(PIECES)):
-            if s == 7:
-                gather(2, 2 * PICKS * J + 0, PICKS * J - LATER, LATER)
             g(s)
             late(s, s < 7)
             if s >= 2:
@@ -265,17 +264,16 @@ def tile_list_dl_prod_gelu_kernel(tc, xT, wgt, w4_words, w4_scales, wd, b, offs,
         for m in range(4):
             low_mm(m)
         for m in range(4):
-            if m < 3:
-                cp(m)
-                pr(m)
-            else:
-                red(m)
+            cp(m)
+            pr(m)
             if m == 1:
                 for i in range(4):
                     high_mm(i)
             fin(0, m)
-        for h in range(2):
-            low_cp(h, h == 0)
+            if m == 0:
+                low_cp(0, True)
+            if m == 3:
+                low_cp(1, False)
         for m in range(3):
             high_pr(m)
             fin(1, m)

@@ -1,7 +1,6 @@
 from contextlib import ExitStack
 
 import concourse.mybir as mybir
-from concourse.masks import make_identity
 
 K, N, T, J = 512, 512, 2048, 512
 FLOPS = 2 * 2 * 2 * K * N * J
@@ -15,17 +14,20 @@ U8 = mybir.dt.uint8
 FP8X4 = mybir.dt.float8_e4m3fn_x4
 FP4X4 = mybir.dt.float4_e2m1fn_x4
 MULT = mybir.AluOpType.mult
-INNER = mybir.AxisListType.X
 GELU = mybir.ActivationFunctionType.Gelu_apprx_tanh
 
 P = 128
 PACK = 4
 PICKS = 2
-HALF = 256
-RUN = 4
+ENTRIES = PICKS * J
+HALF = J // 2
 W = 128
-LATER = 0
-PIECES = [(0, 0, W), (1, 0, W), (0, W, W), (1, W, W), (0, 2 * W, W), (0, 3 * W, W), (1, 2 * W, W), (1, 3 * W, W)]
+BLOCKS = N // P
+RUN = 4
+LAG = 2
+PIECES = [(c, j0) for j0 in (0, W) for c in range(PICKS)] + [(c, j0) for c in range(PICKS) for j0 in (HALF, HALF + W)]
+LAST = len(PIECES) - 1
+WARM_PIECE = LAST - 1
 
 
 def tile_list_dl_prod_gelu_kernel(tc, xT, wgt, w4_words, w4_scales, wd, b, offs, out):
@@ -34,33 +36,44 @@ def tile_list_dl_prod_gelu_kernel(tc, xT, wgt, w4_words, w4_scales, wd, b, offs,
         pool = ctx.enter_context(tc.tile_pool(name="sbuf", bufs=1))
         psum = ctx.enter_context(tc.psum_pool(name="psum", bufs=1))
 
-        offsets = pool.tile([P, PICKS * J // 16], U16, name="offsets")
-        weights = pool.tile([P, PICKS * J], F32, name="weights", align_bytes=64)
+        offsets = pool.tile([P, ENTRIES // 16], U16, name="offsets")
+        weights = pool.tile([P, ENTRIES], F32, name="weights", align_bytes=64)
         plane = [pool.tile([P, T], F32, name="plane%d" % t) for t in range(PACK)]
         w4_codes = pool.tile([P, 2 * N], U8, name="w4_codes", align_bytes=64)
         w4_scale = pool.tile([P, N], U8, name="w4_scale", align_bytes=64)
-        bias = pool.tile([P, N // P], F32, name="bias")
-        OWN = 3 * PICKS * J
-        RAW = OWN + PICKS * J
-        stage = pool.tile([P, RAW + 2 * PACK * HALF + 0], F32, name="stage")
-        wd_raw = [stage[:, RAW + u * PACK * HALF : RAW + (u + 1) * PACK * HALF].rearrange("p (t n) -> p t n", t=PACK) for u in range(2)]
+        bias = pool.tile([P, BLOCKS], F32, name="bias")
+        slots_at = (PACK - 1) * ENTRIES
+        raw_at = slots_at + ENTRIES
+        stage = pool.tile([P, raw_at + PACK * N], F32, name="stage")
+        raw_half = [raw_at + u * PACK * HALF for u in range(2)]
+        slot = [slots_at + s * W for s in range(4)] + [slots_at, raw_half[0], raw_half[0] + W, raw_half[1]]
+        a0_first = [raw_half[1] + HALF, raw_half[1] + 2 * HALF, slots_at + 2 * HALF, slots_at + 3 * HALF]
+        wd_raw = [stage[:, raw_half[u] : raw_half[u] + PACK * HALF].rearrange("p (t n) -> p t n", t=PACK) for u in range(2)]
         wd_bf = [pool.tile([P, HALF, PACK], BF16, name="wd_bf%d" % u, align_bytes=64) for u in range(2)]
         wd_codes = [pool.tile([P, HALF], U32, name="wd_codes%d" % u, align_bytes=64) for u in range(2)]
         wd_scale = [pool.tile([P, HALF], U8, name="wd_scale%d" % u, align_bytes=64) for u in range(2)]
         x_bf = [pool.tile([P, J, PACK], BF16, name="x_bf%d" % v, align_bytes=64) for v in range(2)]
         x_codes = [pool.tile([P, J], U32, name="x_codes%d" % v, align_bytes=64) for v in range(2)]
         x_scale = [pool.tile([P, J], U8, name="x_scale%d" % v, align_bytes=64) for v in range(2)]
-        both = [psum.tile([P, J], F32, name="bank%d" % m) for m in range(4)]
-        low = [psum.tile([P, J], F32, name="low%d" % h) for h in range(2)]
-        high = [psum.tile([P, J], F32, name="high%d" % m) for m in range(2)]
-        slot = [OWN, OWN + W, OWN + 2 * W, OWN + 3 * W, OWN, RAW, RAW+W, RAW + 8*W]
+        both = [psum.tile([P, J], F32, name="bank%d" % m) for m in range(BLOCKS)]
+        a0_bank = [psum.tile([P, J], F32, name="a0_bank%d" % h) for h in range(2)]
+        a1_bank = [psum.tile([P, J], F32, name="a1_bank%d" % m) for m in range(2)]
+        a0_second = [pool.tile([P, J], F32, name="a0_second%d" % h) for h in range(2)]
+        prod = {(v, m): pool.tile([P, HALF], F32, name="prod%d_%d" % (v, m)) for v in range(2) for m in range(BLOCKS)}
+        res = {(v, m): pool.tile([P, HALF], F32, name="res%d_%d" % (v, m)) for v in range(2) for m in range(BLOCKS)}
 
         x_rows = xT.rearrange("(p t) c -> p t c", t=PACK)
         wd_rows = wd.rearrange("(p t) n -> p t n", t=PACK)
 
+        def copy(on_scalar, dst, src):
+            if on_scalar:
+                nc.scalar.copy(dst, src)
+            else:
+                nc.vector.tensor_copy(dst, src)
+
         rows = pool.tile([P, 64], F32, name="rows", align_bytes=64)
         cols = pool.tile([P, 2, 32], F32, name="cols", align_bytes=64)
-        spread = [pool.tile([P, 8, 2, 2, 16], F32, name="spread%d" % k, align_bytes=64) for k in range(PICKS)]
+        spread = [pool.tile([P, 8, 2, 2, 16], F32, name="spread%d" % c, align_bytes=64) for c in range(PICKS)]
         nc.sync.dma_start(rows[:], wgt[0:P:16, :].rearrange("g (a c) -> g a c", c=64))
 
         nc.vector.memset(w4_scale[:].bitcast(I32), 0)
@@ -69,179 +82,122 @@ def tile_list_dl_prod_gelu_kernel(tc, xT, wgt, w4_words, w4_scales, wd, b, offs,
         nc.vector.memset(zero[:], 0.0)
         nc.scalar.activation(warm[:], zero[:], GELU)
 
-        def copy(on_scalar, dst, src):
-            if on_scalar:
-                nc.scalar.copy(dst, src)
-            else:
-                nc.vector.tensor_copy(dst, src)
-
         for u in range(2):
             nc.vector.transpose(cols[:, u, :], rows[:, 32 * u : 32 * u + 32])
-        for k in range(PICKS):
-            src = cols[:].rearrange("p u (g a) -> p a u g", g=2)[:, 8 * k : 8 * k + 8, :, :].unsqueeze(4).to_broadcast([P, 8, 2, 2, 16])
-            copy(k == 1, spread[k][:], src)
-        for k in range(PICKS):
-            nc.vector.transpose(weights[:, k * J : (k + 1) * J], spread[k][:].rearrange("p a u g r -> p (a u g r)"))
+        for c in range(PICKS):
+            src = cols[:].rearrange("p u (h a) -> p a u h", h=2)[:, 8 * c : 8 * c + 8, :, :].unsqueeze(4).to_broadcast([P, 8, 2, 2, 16])
+            copy(c == 1, spread[c][:], src)
+        for c in range(PICKS):
+            nc.vector.transpose(weights[:, c * J : (c + 1) * J], spread[c][:].rearrange("p a u h r -> p (a u h r)"))
 
-        def load_plane(t):
-            nc.sync.dma_start(plane[t][:], x_rows[:, t, :])
+        for quad in range(4):
+            nc.scalar.dma_start(
+                w4_scale[:].bitcast(I32)[32 * quad : 32 * quad + 4, :],
+                w4_scales[0].bitcast(I32)[4 * quad : 4 * quad + 4, :],
+            )
 
-        def load_scales(eng=nc.sync):
-            for q in range(4):
-                eng.dma_start(
-                    w4_scale[:].bitcast(I32)[32 * q : 32 * q + 4, :],
-                    w4_scales[0].bitcast(I32)[4 * q : 4 * q + 4, :],
-                )
-
-        def load_w4():
-            nc.sync.dma_start(w4_codes[:].bitcast(I32), w4_words[0].bitcast(I32))
-
-        def load_wd(u):
-            nc.sync.dma_start(wd_raw[u], wd_rows[:, :, u * HALF : (u + 1) * HALF])
-
-        def load_bias(eng=nc.sync):
-            with nc.allow_non_contiguous_dma(reason="one bias value to a partition"):
-                eng.dma_start(bias[:], b.rearrange("(m p) -> p m", p=P))
-
-        load_scales(nc.scalar)
-        load_plane(0)
+        nc.sync.dma_start(plane[0][:], x_rows[:, 0, :])
         nc.sync.dma_start(offsets[:], offs)
-        load_plane(1)
-        load_plane(2)
-        load_w4()
-        load_plane(3)
-        load_wd(0)
-        load_wd(1)
-        load_bias()
+        for t in range(1, PACK):
+            if t == PACK - 1:
+                nc.sync.dma_start(w4_codes[:].bitcast(I32), w4_words[0].bitcast(I32))
+            nc.sync.dma_start(plane[t][:], x_rows[:, t, :])
+        for u in range(2):
+            nc.sync.dma_start(wd_raw[u], wd_rows[:, :, u * HALF : (u + 1) * HALF])
+        with nc.allow_non_contiguous_dma(reason="one bias value to a partition"):
+            nc.sync.dma_start(bias[:], b.rearrange("(m p) -> p m", p=P))
 
         def gather(t, at, e0, n):
-            nc.vector.tensor_tensor(stage[:, at : at + n], plane[t][:].indirect(offsets[:, e0 // 16 : (e0 + n) // 16]), weights[:, e0 : e0 + n], MULT)
+            window = plane[t][:].indirect(offsets[:, e0 // 16 : (e0 + n) // 16])
+            nc.vector.tensor_tensor(stage[:, at : at + n], window, weights[:, e0 : e0 + n], MULT)
 
-        def where(s):
-            k, j0, w = PIECES[s]
-            return j0 // HALF, k * HALF + j0 % HALF, w
+        def entry(s):
+            c, j0 = PIECES[s]
+            return c * J + j0
 
-        def pair(on_scalar, v, c0, w, first, second, t0):
-            step = (second - first) // w
-            src = stage[:, first : first + (step + 1) * w].rearrange("p (x w) -> p x w", w=w)[:, 0 : step + 1 : step, :]
-            copy(on_scalar, x_bf[v][:, c0 : c0 + w, t0 : t0 + 2], src.rearrange("p t w -> p w t"))
+        def column(s):
+            c, j0 = PIECES[s]
+            return j0 // HALF, c * HALF + j0 % HALF
 
-        def early(s):
-            k, j0, w = PIECES[s]
-            v, c0, w = where(s)
-            pair(True, v, c0, w, k * J + j0, PICKS * J + k * J + j0, 0)
+        def lay_pair(on_scalar, s, first, second, t0):
+            v, c0 = column(s)
+            step = (second - first) // W
+            src = stage[:, first : second + W].rearrange("p (x w) -> p x w", w=W)[:, 0 : step + 1 : step, :]
+            copy(on_scalar, x_bf[v][:, c0 : c0 + W, t0 : t0 + 2], src.rearrange("p t w -> p w t"))
 
-        def g(s):
-            k, j0, w = PIECES[s]
-            gather(PACK - 1, slot[s], k * J + j0, w)
+        def quantize(codes, scale, src):
+            nc.vector.quantize_mx(codes.bitcast(FP8X4), scale, src.rearrange("p w t -> p (w t)"))
 
-        def late(s, on_scalar):
-            k, j0, w = PIECES[s]
-            v, c0, w = where(s)
-            e0 = k * J + j0
-            pair(on_scalar, v, c0, w, 2 * PICKS * J + e0, slot[s], 2)
+        def quantize_x(s):
+            v, c0 = column(s)
+            quantize(x_codes[v][:, c0 : c0 + W], x_scale[v][:, c0 : c0 + W], x_bf[v][:, c0 : c0 + W, :])
 
-        def quantize(codes, scale, src, w0, w1):
-            nc.vector.quantize_mx(codes[:, w0:w1].bitcast(FP8X4), scale[:, w0:w1], src[:, w0:w1, :].rearrange("p w t -> p (w t)"))
+        def interleave_wd(on_scalar, u):
+            dst = wd_bf[u][:].rearrange("p (g i) t -> p g t i", i=RUN)
+            copy(on_scalar, dst, wd_raw[u].rearrange("p t (g i) -> p g t i", i=RUN))
 
-        def q(s):
-            v, c0, w = where(s)
-            quantize(x_codes[v], x_scale[v], x_bf[v], c0, c0 + w)
+        def quantize_wd(u):
+            quantize(wd_codes[u][:], wd_scale[u][:], wd_bf[u][:])
 
-        def iw(u, on_scalar):
-            copy(on_scalar, wd_bf[u][:].rearrange("p (g i) t -> p g t i", i=RUN), wd_raw[u].rearrange("p t (g i) -> p g t i", i=RUN))
-
-        def qw(u):
-            quantize(wd_codes[u], wd_scale[u], wd_bf[u], 0, HALF)
-
-        def pass_w4(dst, m, v, w0, w1, start):
+        def pass_w4(dst, m, v, c0, start):
             nc.tensor.matmul_mx(
                 dst,
                 lhsT=w4_codes[:, 2 * P * m : 2 * P * (m + 1)].bitcast(FP4X4),
                 lhsT_scale=w4_scale[:, P * m : P * (m + 1)],
-                rhs=x_codes[v][:, w0:w1].bitcast(FP8X4),
-                rhs_scale=x_scale[v][:, w0:w1],
+                rhs=x_codes[v][:, c0 : c0 + W].bitcast(FP8X4),
+                rhs_scale=x_scale[v][:, c0 : c0 + W],
                 start=start,
                 stop=False,
             )
 
-        def pass_wd(dst, m, v, w0, w1):
+        def pass_wd(dst, m, v, c0, n):
             u, mc = m // 2, slice(P * (m % 2), P * (m % 2 + 1))
             nc.tensor.matmul_mx(
                 dst,
                 lhsT=wd_codes[u][:, mc].bitcast(FP8X4),
                 lhsT_scale=wd_scale[u][:, mc],
-                rhs=x_codes[v][:, w0:w1].bitcast(FP8X4),
-                rhs_scale=x_scale[v][:, w0:w1],
+                rhs=x_codes[v][:, c0 : c0 + n].bitcast(FP8X4),
+                rhs_scale=x_scale[v][:, c0 : c0 + n],
                 start=False,
                 stop=True,
             )
 
-        def both_mm(m):
-            for i, c0 in enumerate((0, HALF, W, HALF + W)):
-                pass_w4(both[m][:, c0 : c0 + W], m, 0, c0, c0 + W, i == 0)
+        def project_first(m):
+            for s in range(len(PIECES) // 2):
+                c0 = column(s)[1]
+                pass_w4(both[m][:, c0 : c0 + W], m, 0, c0, s == 0)
             pass_wd(both[m][:], m, 0, 0, J)
 
-        def one_pick(dst, m, k):
-            for e in range(2):
-                pass_w4(dst[:, e * W : (e + 1) * W], m, 1, k * HALF + e * W, k * HALF + (e + 1) * W, e == 0)
-            pass_wd(dst, m, 1, k * HALF, (k + 1) * HALF)
+        def project_second(dst, m, c):
+            for e in range(HALF // W):
+                pass_w4(dst[:, e * W : (e + 1) * W], m, 1, c * HALF + e * W, e == 0)
+            pass_wd(dst, m, 1, c * HALF, HALF)
 
-        def low_mm(m):
-            one_pick(low[m // 2][:, (m % 2) * HALF : (m % 2 + 1) * HALF], m, 0)
+        def product_second(m, j0, j1):
+            a0 = a0_second[m // 2][:, (m % 2) * HALF + j0 : (m % 2) * HALF + j1]
+            nc.vector.tensor_tensor(prod[1, m][:, j0:j1], a1_bank[m][:, j0:j1], a0, MULT)
 
-        def high_mm(m):
-            if m >= 2:
-                high.append(psum.tile([P, J], F32, name="bank%d" % (m - 2)))
-            one_pick(high[m][:, 0:HALF], m, 1)
-
-        prod = {(v, m): pool.tile([P, HALF], F32, name="prod%d_%d" % (v, m)) for v in range(2) for m in range(4)}
-        res = {(v, m): pool.tile([P, HALF], F32, name="res%d_%d" % (v, m)) for v in range(2) for m in range(4)}
-        first = [RAW + 10 * W, RAW + 12 * W, OWN + 4 * W, OWN + 6 * W]
-        first_low = [pool.tile([P, J], F32, name="first_low%d" % h) for h in range(2)]
-
-        def cp(m, on_scalar=True):
-            copy(on_scalar, stage[:, first[m] : first[m] + HALF], both[m][:, 0:HALF])
-
-        def pr(m):
-            nc.vector.tensor_tensor(prod[0, m][:], both[m][:, HALF:J], stage[:, first[m] : first[m] + HALF], MULT)
-
-        def red(m):
-            nc.vector.tensor_reduce(prod[0, m][:], both[m][:].rearrange("p (k w) -> p w k", k=PICKS), INNER, MULT)
-
-        def low_cp(h, on_scalar):
-            copy(on_scalar, first_low[h][:], low[h][:])
-
-        def low_cp1(m, on_scalar):
-            c0 = (m % 2) * HALF
-            copy(on_scalar, first_low[m // 2][:, c0 : c0 + HALF], low[m // 2][:, c0 : c0 + HALF])
-
-        def high_pr(m, j0=0, j1=HALF):
-            nc.vector.tensor_tensor(prod[1, m][:, j0:j1], high[m][:, j0:j1], first_low[m // 2][:, (m % 2) * HALF + j0 : (m % 2) * HALF + j1], MULT)
-
-        def fin(v, m, j0=0, j1=HALF):
+        def finish(v, m, j0, j1):
             nc.scalar.activation(res[v, m][:, j0:j1], prod[v, m][:, j0:j1], GELU, bias=bias[:, m : m + 1])
             nc.sync.dma_start(out[P * m : P * (m + 1), v * HALF + j0 : v * HALF + j1], res[v, m][:, j0:j1])
 
-        warm_in = pool.tile([P, PACK * P], BF16, name="warm_in", align_bytes=64)
+        warm_v, warm_c0 = column(WARM_PIECE)
+        warm_in = x_bf[warm_v][:, warm_c0 : warm_c0 + W, :]
         warm_codes = pool.tile([P, P], U32, name="warm_codes", align_bytes=64)
         warm_scale = pool.tile([P, P], U8, name="warm_scale", align_bytes=64)
-        nc.vector.memset(warm_in[:].bitcast(I32), 0)
-        nc.vector.quantize_mx(warm_codes[:].bitcast(FP8X4), warm_scale[:], warm_in[:])
-        gather(0, 0, 0, PICKS * J)
+        nc.vector.memset(warm_in.rearrange("p w t -> p (w t)").bitcast(I32), 0)
+
+        gather(0, 0, 0, ENTRIES)
         for e0, n in ((0, HALF), (HALF, HALF), (J, J)):
-            gather(1, PICKS * J + e0, e0, n)
-        for k in range(PICKS):
-            for s in range(len(PIECES)):
-                if PIECES[s][0] == k:
-                    early(s)
-        gather(2, 2 * PICKS * J, 0, PICKS * J - LATER)
-        ident = pool.tile([P, P], F32, name="ident")
-        make_identity(nc, ident[:])
-        nc.tensor.transpose(high[1][:, 0:P], plane[PACK - 1][:, 0:P], ident[:])
+            gather(1, ENTRIES + e0, e0, n)
+        for s in sorted(range(len(PIECES)), key=entry):
+            lay_pair(True, s, entry(s), ENTRIES + entry(s), 0)
+        gather(2, 2 * ENTRIES, 0, ENTRIES)
+
+        quantize(warm_codes[:], warm_scale[:], warm_in)
         for n in (J, HALF):
             nc.tensor.matmul_mx(
-                high[1][:, 0:n],
+                a1_bank[1][:, 0:n],
                 lhsT=warm_codes[:].bitcast(FP8X4),
                 lhsT_scale=warm_scale[:],
                 rhs=w4_codes[:, 0 : 2 * n].bitcast(FP4X4),
@@ -249,34 +205,39 @@ def tile_list_dl_prod_gelu_kernel(tc, xT, wgt, w4_words, w4_scales, wd, b, offs,
                 start=True,
                 stop=True,
             )
+
         for u in range(2):
-            iw(u, u == 1)
-            qw(u)
+            interleave_wd(u == 1, u)
+            quantize_wd(u)
         for s in range(len(PIECES)):
-            g(s)
-            late(s, s < 7)
-            if s >= 2:
-                q(s - 2)
-        for s in range(len(PIECES) - 2, len(PIECES)):
-            q(s)
-        for m in range(4):
-            both_mm(m)
-        for m in range(4):
-            low_mm(m)
-        for m in range(4):
-            cp(m)
-            pr(m)
+            gather(PACK - 1, slot[s], entry(s), W)
+            lay_pair(s < LAST, s, 2 * ENTRIES + entry(s), slot[s], 2)
+            if s >= LAG:
+                quantize_x(s - LAG)
+        for s in range(len(PIECES) - LAG, len(PIECES)):
+            quantize_x(s)
+
+        for m in range(BLOCKS):
+            project_first(m)
+        for m in range(BLOCKS):
+            project_second(a0_bank[m // 2][:, (m % 2) * HALF : (m % 2 + 1) * HALF], m, 0)
+
+        for m in range(BLOCKS):
+            a0 = stage[:, a0_first[m] : a0_first[m] + HALF]
+            nc.scalar.copy(a0, both[m][:, 0:HALF])
+            nc.vector.tensor_tensor(prod[0, m][:], both[m][:, HALF:J], a0, MULT)
             if m == 1:
-                for i in range(4):
-                    high_mm(i)
-            fin(0, m)
+                a1_bank.extend([psum.tile([P, J], F32, name="bank%d" % e) for e in range(2)])
+                for m2 in range(BLOCKS):
+                    project_second(a1_bank[m2][:, 0:HALF], m2, 1)
+            finish(0, m, 0, HALF)
             if m == 0:
-                low_cp(0, True)
-            if m == 3:
-                low_cp(1, False)
-        for m in range(3):
-            high_pr(m)
-            fin(1, m)
+                nc.scalar.copy(a0_second[0][:], a0_bank[0][:])
+            if m == BLOCKS - 1:
+                nc.vector.tensor_copy(a0_second[1][:], a0_bank[1][:])
+        for m in range(BLOCKS - 1):
+            product_second(m, 0, HALF)
+            finish(1, m, 0, HALF)
         for j0 in (0, W):
-            high_pr(3, j0, j0 + W)
-            fin(1, 3, j0, j0 + W)
+            product_second(BLOCKS - 1, j0, j0 + W)
+            finish(1, BLOCKS - 1, j0, j0 + W)

@@ -28,6 +28,8 @@ LAG = 2
 PIECES = [(c, j0) for j0 in (0, W) for c in range(PICKS)] + [(c, j0) for c in range(PICKS) for j0 in (HALF, HALF + W)]
 LAST = len(PIECES) - 1
 WARM_PIECE = LAST - 1
+WARM_M = 32
+WARM_PASSES = 4
 
 
 def tile_list_dl_prod_gelu_kernel(tc, xT, wgt, w4_words, w4_scales, wd, b, offs, out):
@@ -182,10 +184,11 @@ def tile_list_dl_prod_gelu_kernel(tc, xT, wgt, w4_words, w4_scales, wd, b, offs,
             nc.sync.dma_start(out[P * m : P * (m + 1), v * HALF + j0 : v * HALF + j1], res[v, m][:, j0:j1])
 
         warm_v, warm_c0 = column(WARM_PIECE)
-        warm_in = x_bf[warm_v][:, warm_c0 : warm_c0 + W, :]
-        warm_codes = pool.tile([P, P], U32, name="warm_codes", align_bytes=64)
-        warm_scale = pool.tile([P, P], U8, name="warm_scale", align_bytes=64)
+        warm_in = x_bf[warm_v][:, warm_c0 : warm_c0 + WARM_M, :]
+        warm_codes = pool.tile([P, J], U32, name="warm_codes", align_bytes=64)
+        warm_scale = pool.tile([P, WARM_M], U8, name="warm_scale", align_bytes=64)
         nc.vector.memset(warm_in.rearrange("p w t -> p (w t)").bitcast(I32), 0)
+        nc.vector.memset(warm_codes[:], 0)
 
         gather(0, 0, 0, ENTRIES)
         for e0, n in ((0, HALF), (HALF, HALF), (J, J)):
@@ -194,14 +197,14 @@ def tile_list_dl_prod_gelu_kernel(tc, xT, wgt, w4_words, w4_scales, wd, b, offs,
             lay_pair(True, s, entry(s), ENTRIES + entry(s), 0)
         gather(2, 2 * ENTRIES, 0, ENTRIES)
 
-        quantize(warm_codes[:], warm_scale[:], warm_in)
-        for n in (J, HALF):
+        quantize(warm_codes[:, 0:WARM_M], warm_scale[:], warm_in)
+        for e in range(WARM_PASSES):
             nc.tensor.matmul_mx(
-                a1_bank[1][:, 0:n],
-                lhsT=warm_codes[:].bitcast(FP8X4),
+                a1_bank[1][0:WARM_M, :],
+                lhsT=warm_codes[:, 0:WARM_M].bitcast(FP8X4),
                 lhsT_scale=warm_scale[:],
-                rhs=w4_codes[:, 0 : 2 * n].bitcast(FP4X4),
-                rhs_scale=w4_scale[:, 0:n],
+                rhs=warm_codes[:].bitcast(FP8X4),
+                rhs_scale=w4_scale[:],
                 start=True,
                 stop=True,
             )

@@ -27,9 +27,6 @@ RUN = 4
 LAG = 2
 PIECES = [(c, j0) for j0 in (0, W) for c in range(PICKS)] + [(c, j0) for c in range(PICKS) for j0 in (HALF, HALF + W)]
 LAST = len(PIECES) - 1
-WARM_PIECE = LAST - 1
-WARM_M = 32
-WARM_PASSES = 4
 
 
 def tile_list_dl_prod_gelu_kernel(tc, xT, wgt, w4_words, w4_scales, wd, b, offs, out):
@@ -183,31 +180,12 @@ def tile_list_dl_prod_gelu_kernel(tc, xT, wgt, w4_words, w4_scales, wd, b, offs,
             nc.scalar.activation(res[v, m][:, j0:j1], prod[v, m][:, j0:j1], GELU, bias=bias[:, m : m + 1])
             nc.sync.dma_start(out[P * m : P * (m + 1), v * HALF + j0 : v * HALF + j1], res[v, m][:, j0:j1])
 
-        warm_v, warm_c0 = column(WARM_PIECE)
-        warm_in = x_bf[warm_v][:, warm_c0 : warm_c0 + WARM_M, :]
-        warm_codes = pool.tile([P, J], U32, name="warm_codes", align_bytes=64)
-        warm_scale = pool.tile([P, WARM_M], U8, name="warm_scale", align_bytes=64)
-        nc.vector.memset(warm_in.rearrange("p w t -> p (w t)").bitcast(I32), 0)
-        nc.vector.memset(warm_codes[:], 0)
-
         gather(0, 0, 0, ENTRIES)
         for e0, n in ((0, HALF), (HALF, HALF), (J, J)):
             gather(1, ENTRIES + e0, e0, n)
         for s in sorted(range(len(PIECES)), key=entry):
             lay_pair(True, s, entry(s), ENTRIES + entry(s), 0)
         gather(2, 2 * ENTRIES, 0, ENTRIES)
-
-        quantize(warm_codes[:, 0:WARM_M], warm_scale[:], warm_in)
-        for e in range(WARM_PASSES):
-            nc.tensor.matmul_mx(
-                a1_bank[1][0:WARM_M, :],
-                lhsT=warm_codes[:, 0:WARM_M].bitcast(FP8X4),
-                lhsT_scale=warm_scale[:],
-                rhs=warm_codes[:].bitcast(FP8X4),
-                rhs_scale=w4_scale[:],
-                start=True,
-                stop=True,
-            )
 
         for u in range(2):
             interleave_wd(u == 1, u)

from contextlib import ExitStack

import concourse.mybir as mybir

K, N, T, J = 512, 512, 2048, 512
FLOPS = 2 * 2 * 2 * K * N * J

F32 = mybir.dt.float32
BF16 = mybir.dt.bfloat16
I32 = mybir.dt.int32
U32 = mybir.dt.uint32
U16 = mybir.dt.uint16
U8 = mybir.dt.uint8
FP8X4 = mybir.dt.float8_e4m3fn_x4
FP4X4 = mybir.dt.float4_e2m1fn_x4
MULT = mybir.AluOpType.mult
GELU = mybir.ActivationFunctionType.Gelu_apprx_tanh

P = 128
PACK = 4
PICKS = 2
ENTRIES = PICKS * J
HALF = J // 2
W = 128
BLOCKS = N // P
RUN = 4
LAG = 2
PIECES = [(c, j0) for j0 in (0, W) for c in range(PICKS)] + [(c, j0) for c in range(PICKS) for j0 in (HALF, HALF + W)]
LAST = len(PIECES) - 1


def tile_list_dl_prod_gelu_kernel(tc, xT, wgt, w4_words, w4_scales, wd, b, offs, out):
    nc = tc.nc
    with ExitStack() as ctx:
        pool = ctx.enter_context(tc.tile_pool(name="sbuf", bufs=1))
        psum = ctx.enter_context(tc.psum_pool(name="psum", bufs=1))

        offsets = pool.tile([P, ENTRIES // 16], U16, name="offsets")
        weights = pool.tile([P, ENTRIES], F32, name="weights", align_bytes=64)
        plane = [pool.tile([P, T], F32, name="plane%d" % t) for t in range(PACK)]
        w4_codes = pool.tile([P, 2 * N], U8, name="w4_codes", align_bytes=64)
        w4_scale = pool.tile([P, N], U8, name="w4_scale", align_bytes=64)
        bias = pool.tile([P, BLOCKS], F32, name="bias")
        slots_at = (PACK - 1) * ENTRIES
        raw_at = slots_at + ENTRIES
        stage = pool.tile([P, raw_at + PACK * N], F32, name="stage")
        raw_half = [raw_at + u * PACK * HALF for u in range(2)]
        slot = [slots_at + s * W for s in range(4)] + [slots_at, raw_half[0], raw_half[0] + W, raw_half[1]]
        a0_first = [raw_half[1] + HALF, raw_half[1] + 2 * HALF, slots_at + 2 * HALF, slots_at + 3 * HALF]
        wd_raw = [stage[:, raw_half[u] : raw_half[u] + PACK * HALF].rearrange("p (t n) -> p t n", t=PACK) for u in range(2)]
        wd_bf = [pool.tile([P, HALF, PACK], BF16, name="wd_bf%d" % u, align_bytes=64) for u in range(2)]
        wd_codes = [pool.tile([P, HALF], U32, name="wd_codes%d" % u, align_bytes=64) for u in range(2)]
        wd_scale = [pool.tile([P, HALF], U8, name="wd_scale%d" % u, align_bytes=64) for u in range(2)]
        x_bf = [pool.tile([P, J, PACK], BF16, name="x_bf%d" % v, align_bytes=64) for v in range(2)]
        x_codes = [pool.tile([P, J], U32, name="x_codes%d" % v, align_bytes=64) for v in range(2)]
        x_scale = [pool.tile([P, J], U8, name="x_scale%d" % v, align_bytes=64) for v in range(2)]
        both = [psum.tile([P, J], F32, name="bank%d" % m) for m in range(BLOCKS)]
        a0_bank = [psum.tile([P, J], F32, name="a0_bank%d" % h) for h in range(2)]
        a1_bank = [psum.tile([P, J], F32, name="a1_bank%d" % m) for m in range(2)]
        a0_second = [pool.tile([P, J], F32, name="a0_second%d" % h) for h in range(2)]
        prod = {(v, m): pool.tile([P, HALF], F32, name="prod%d_%d" % (v, m)) for v in range(2) for m in range(BLOCKS)}
        res = {(v, m): pool.tile([P, HALF], F32, name="res%d_%d" % (v, m)) for v in range(2) for m in range(BLOCKS)}

        x_rows = xT.rearrange("(p t) c -> p t c", t=PACK)
        wd_rows = wd.rearrange("(p t) n -> p t n", t=PACK)

        def copy(on_scalar, dst, src):
            if on_scalar:
                nc.scalar.copy(dst, src)
            else:
                nc.vector.tensor_copy(dst, src)

        rows = pool.tile([P, 64], F32, name="rows", align_bytes=64)
        cols = pool.tile([P, 2, 32], F32, name="cols", align_bytes=64)
        spread = [pool.tile([P, 8, 2, 2, 16], F32, name="spread%d" % c, align_bytes=64) for c in range(PICKS)]
        nc.sync.dma_start(rows[:], wgt[0:P:16, :].rearrange("g (a c) -> g a c", c=64))

        nc.vector.memset(w4_scale[:].bitcast(I32), 0)
        zero = pool.tile([P, 1], F32, name="zero")
        warm = pool.tile([P, 1], F32, name="warm")
        nc.vector.memset(zero[:], 0.0)
        nc.scalar.activation(warm[:], zero[:], GELU)

        for u in range(2):
            nc.vector.transpose(cols[:, u, :], rows[:, 32 * u : 32 * u + 32])
        for c in range(PICKS):
            src = cols[:].rearrange("p u (h a) -> p a u h", h=2)[:, 8 * c : 8 * c + 8, :, :].unsqueeze(4).to_broadcast([P, 8, 2, 2, 16])
            copy(c == 1, spread[c][:], src)
        for c in range(PICKS):
            nc.vector.transpose(weights[:, c * J : (c + 1) * J], spread[c][:].rearrange("p a u h r -> p (a u h r)"))

        for quad in range(4):
            nc.scalar.dma_start(
                w4_scale[:].bitcast(I32)[32 * quad : 32 * quad + 4, :],
                w4_scales[0].bitcast(I32)[4 * quad : 4 * quad + 4, :],
            )

        nc.sync.dma_start(plane[0][:], x_rows[:, 0, :])
        nc.sync.dma_start(offsets[:], offs)
        for t in range(1, PACK):
            if t == PACK - 1:
                nc.sync.dma_start(w4_codes[:].bitcast(I32), w4_words[0].bitcast(I32))
            nc.sync.dma_start(plane[t][:], x_rows[:, t, :])
        for u in range(2):
            nc.sync.dma_start(wd_raw[u], wd_rows[:, :, u * HALF : (u + 1) * HALF])
        with nc.allow_non_contiguous_dma(reason="one bias value to a partition"):
            nc.sync.dma_start(bias[:], b.rearrange("(m p) -> p m", p=P))

        def gather(t, at, e0, n):
            window = plane[t][:].indirect(offsets[:, e0 // 16 : (e0 + n) // 16])
            nc.vector.tensor_tensor(stage[:, at : at + n], window, weights[:, e0 : e0 + n], MULT)

        def entry(s):
            c, j0 = PIECES[s]
            return c * J + j0

        def column(s):
            c, j0 = PIECES[s]
            return j0 // HALF, c * HALF + j0 % HALF

        def lay_pair(on_scalar, s, first, second, t0):
            v, c0 = column(s)
            step = (second - first) // W
            src = stage[:, first : second + W].rearrange("p (x w) -> p x w", w=W)[:, 0 : step + 1 : step, :]
            copy(on_scalar, x_bf[v][:, c0 : c0 + W, t0 : t0 + 2], src.rearrange("p t w -> p w t"))

        def quantize(codes, scale, src):
            nc.vector.quantize_mx(codes.bitcast(FP8X4), scale, src.rearrange("p w t -> p (w t)"))

        def quantize_x(s):
            v, c0 = column(s)
            quantize(x_codes[v][:, c0 : c0 + W], x_scale[v][:, c0 : c0 + W], x_bf[v][:, c0 : c0 + W, :])

        def interleave_wd(on_scalar, u):
            dst = wd_bf[u][:].rearrange("p (g i) t -> p g t i", i=RUN)
            copy(on_scalar, dst, wd_raw[u].rearrange("p t (g i) -> p g t i", i=RUN))

        def quantize_wd(u):
            quantize(wd_codes[u][:], wd_scale[u][:], wd_bf[u][:])

        def pass_w4(dst, m, v, c0, start):
            nc.tensor.matmul_mx(
                dst,
                lhsT=w4_codes[:, 2 * P * m : 2 * P * (m + 1)].bitcast(FP4X4),
                lhsT_scale=w4_scale[:, P * m : P * (m + 1)],
                rhs=x_codes[v][:, c0 : c0 + W].bitcast(FP8X4),
                rhs_scale=x_scale[v][:, c0 : c0 + W],
                start=start,
                stop=False,
            )

        def pass_wd(dst, m, v, c0, n):
            u, mc = m // 2, slice(P * (m % 2), P * (m % 2 + 1))
            nc.tensor.matmul_mx(
                dst,
                lhsT=wd_codes[u][:, mc].bitcast(FP8X4),
                lhsT_scale=wd_scale[u][:, mc],
                rhs=x_codes[v][:, c0 : c0 + n].bitcast(FP8X4),
                rhs_scale=x_scale[v][:, c0 : c0 + n],
                start=False,
                stop=True,
            )

        def project_first(m):
            for s in range(len(PIECES) // 2):
                c0 = column(s)[1]
                pass_w4(both[m][:, c0 : c0 + W], m, 0, c0, s == 0)
            pass_wd(both[m][:], m, 0, 0, J)

        def project_second(dst, m, c):
            for e in range(HALF // W):
                pass_w4(dst[:, e * W : (e + 1) * W], m, 1, c * HALF + e * W, e == 0)
            pass_wd(dst, m, 1, c * HALF, HALF)

        def product_second(m, j0, j1):
            a0 = a0_second[m // 2][:, (m % 2) * HALF + j0 : (m % 2) * HALF + j1]
            nc.vector.tensor_tensor(prod[1, m][:, j0:j1], a1_bank[m][:, j0:j1], a0, MULT)

        def finish(v, m, j0, j1):
            nc.scalar.activation(res[v, m][:, j0:j1], prod[v, m][:, j0:j1], GELU, bias=bias[:, m : m + 1])
            nc.sync.dma_start(out[P * m : P * (m + 1), v * HALF + j0 : v * HALF + j1], res[v, m][:, j0:j1])

        gather(0, 0, 0, ENTRIES)
        for e0, n in ((0, HALF), (HALF, HALF), (J, J)):
            gather(1, ENTRIES + e0, e0, n)
        for s in sorted(range(len(PIECES)), key=entry):
            lay_pair(True, s, entry(s), ENTRIES + entry(s), 0)
        gather(2, 2 * ENTRIES, 0, ENTRIES)

        for u in range(2):
            interleave_wd(u == 1, u)
            quantize_wd(u)
        for s in range(len(PIECES)):
            gather(PACK - 1, slot[s], entry(s), W)
            lay_pair(s < LAST, s, 2 * ENTRIES + entry(s), slot[s], 2)
            if s >= LAG:
                quantize_x(s - LAG)
        for s in range(len(PIECES) - LAG, len(PIECES)):
            quantize_x(s)

        for m in range(BLOCKS):
            project_first(m)
        for m in range(BLOCKS):
            project_second(a0_bank[m // 2][:, (m % 2) * HALF : (m % 2 + 1) * HALF], m, 0)

        for m in range(BLOCKS):
            a0 = stage[:, a0_first[m] : a0_first[m] + HALF]
            nc.scalar.copy(a0, both[m][:, 0:HALF])
            nc.vector.tensor_tensor(prod[0, m][:], both[m][:, HALF:J], a0, MULT)
            if m == 1:
                a1_bank.extend([psum.tile([P, J], F32, name="bank%d" % e) for e in range(2)])
                for m2 in range(BLOCKS):
                    project_second(a1_bank[m2][:, 0:HALF], m2, 1)
            finish(0, m, 0, HALF)
            if m == 0:
                nc.scalar.copy(a0_second[0][:], a0_bank[0][:])
            if m == BLOCKS - 1:
                nc.vector.tensor_copy(a0_second[1][:], a0_bank[1][:])
        for m in range(BLOCKS - 1):
            product_second(m, 0, HALF)
            finish(1, m, 0, HALF)
        for j0 in (0, W):
            product_second(BLOCKS - 1, j0, j0 + W)
            finish(1, BLOCKS - 1, j0, j0 + W)
